import numpy as np
import ml_dtypes


def mxq(x, axis, fmt="e4m3"):
    dtype, down = {"e4m3": (ml_dtypes.float8_e4m3fn, 7), "e5m2": (ml_dtypes.float8_e5m2, 14)}[fmt]
    v = np.moveaxis(np.asarray(x, np.float32).astype(ml_dtypes.bfloat16).astype(np.float64), axis, -1)
    blocks = v.reshape(v.shape[:-1] + (-1, 32))
    amax = np.abs(blocks).max(-1, keepdims=True)
    byte = np.maximum(np.where(amax > 0, np.frexp(amax)[1] - 1 + 127, 0) - down, 1)
    scale = np.exp2(byte - 127.0)
    codes = (blocks / scale).astype(np.float32).astype(dtype).astype(np.float64)
    return np.moveaxis((codes * scale).reshape(v.shape), -1, axis)


WIDE = False


def mx_kscale(k):
    if not WIDE:
        return np.ones(k)
    levels = np.array([24, -24, 12, -12, 0])
    if k % 512:
        return np.exp2(np.random.permutation(np.resize(levels, k // 32))).repeat(32)
    a = np.empty((k // 512, 16))
    for p in range(k // 512):
        a[p, :8] = np.random.permutation(np.resize(levels, 8))
        for g in range(8):
            far = levels[np.abs(levels - a[p, g]) >= 10]
            a[p, g + 8] = far[np.random.randint(len(far))]
    return np.exp2(a.ravel()).repeat(32)


def f64(x):
    return np.asarray(x).astype(np.float64)


def striped8(idx):
    return np.concatenate([v.reshape(-1, 16).T for v in idx]).astype(np.uint16)


def unstriped8(offs):
    return np.stack([offs[16 * g:16 * g + 16].T.reshape(-1) for g in range(8)]).astype(np.int64)


E2M1 = np.array([0.0, 0.5, 1.0, 1.5, 2.0, 3.0, 4.0, 6.0, -0.0, -0.5, -1.0, -1.5, -2.0, -3.0, -4.0, -6.0])


def pack_weight(w, fmt):
    k, n = w.shape
    w = f64(np.asarray(w, np.float32).astype(ml_dtypes.bfloat16)).reshape(k // 32, 32, n)
    amax = np.abs(w).max(1)
    if fmt == "e4m3":
        byte = np.frexp(amax)[1] - 1 + 127 - 7
    else:
        mant, ex = np.frexp(amax / 6.0)
        byte = np.where(mant > 0.5, ex, ex - 1) + 127
    byte = np.clip(np.where(amax > 0, byte, 1), 1, 254)
    scaled = (w * np.exp2(127.0 - byte)[:, None, :]).reshape(k, n).astype(np.float32)
    by_word = np.ascontiguousarray(scaled.reshape(k // 512, 128, 4, n).transpose(0, 1, 3, 2))
    if fmt == "e4m3":
        words = by_word.astype(ml_dtypes.float8_e4m3fn).view(np.uint8)
    else:
        c = by_word.astype(ml_dtypes.float4_e2m1fn).view(np.uint8) & 0xF
        words = (c[..., 0::2] | (c[..., 1::2] << 4)).reshape(k // 512, 128, 2 * n)
    return np.ascontiguousarray(words), np.ascontiguousarray(byte.astype(np.uint8).reshape(k // 512, 16, n))


def unpack_weight(words, scales, fmt):
    g, _, n = scales.shape
    words = np.ascontiguousarray(words).reshape(g, 128, n, -1)
    if fmt == "e4m3":
        vals = words.view(ml_dtypes.float8_e4m3fn).astype(np.float64)
    else:
        nib = np.empty((g, 128, n, 4), np.uint8)
        nib[..., 0::2] = words & 0xF
        nib[..., 1::2] = words >> 4
        vals = E2M1[nib]
    vals = vals * np.repeat(np.exp2(scales.astype(np.float64) - 127.0), 8, axis=1)[..., None]
    return vals.transpose(0, 1, 3, 2).reshape(g * 512, n)


def sigm(f):
    return 1.0 / (1.0 + np.exp(-np.maximum(f, -700.0)))


K, N, T, J = 512, 512, 2048, 1024


def setup_inputs():
    n = np.random.standard_normal
    s = mx_kscale(K)[:, None]
    p_wk = pack_weight(n((K, N)) / np.sqrt(K) / s, "e4m3")
    p_wv = pack_weight(n((K, N)) / np.sqrt(K) / s, "e2m1")
    return {
        "xT": (n((K, T)) * s).astype(np.float32),
        "wgt": np.repeat(np.random.uniform(0.5, 2.0, (8, J)), 16, axis=0).astype(np.float32),
        "wk_words": p_wk[0],
        "wk_scales": p_wk[1],
        "wv_words": p_wv[0],
        "wv_scales": p_wv[1],
        "st": (n((N, J))).astype(np.float32),
        "wgo": np.repeat(np.random.uniform(0.5, 2.0, (8, J)), 16, axis=0).astype(np.float32),
        "offs": striped8(np.stack([np.random.permutation(T)[:J] for _ in range(8)])),
        "offs2": striped8(np.stack([np.random.permutation(T)[:J] for _ in range(8)])),
    }


def reference(xT, wgt, wk_words, wk_scales, wv_words, wv_scales, st, wgo, offs, offs2):
    idx = unstriped8(offs)
    idx2 = unstriped8(offs2)
    rows = np.arange(K)
    xg = f64(wgt)[rows // 4 % 128] * f64(xT)[rows[:, None], idx[rows % 512 // 64]]
    xT_ = mxq(xg, 0, "e4m3")
    wk_ = unpack_weight(wk_words, wk_scales, "e4m3")
    wv_ = unpack_weight(wv_words, wv_scales, "e2m1")
    ke = wk_.T @ xT_
    ve = wv_.T @ xT_
    gate = sigm(ke * f64(st))
    out = np.zeros((N, T))
    rows = np.arange(N)
    out[rows[:, None], idx2[rows % 128 // 16]] = f64(wgo)[rows % 128] * (gate * ve)
    return out

@@ -1,0 +1,128 @@
+from contextlib import ExitStack
+
+import concourse.mybir as mybir
+
+K, N, T, J = 512, 512, 2048, 1024
+P = 128
+PACK = 4
+BLOCKS = N // P
+CHUNKS = ((0, 256), (256, 512), (512, 1024))
+FLOPS = 2 * 2 * K * N * J
+
+F32 = mybir.dt.float32
+BF16 = mybir.dt.bfloat16
+I32 = mybir.dt.int32
+U32 = mybir.dt.uint32
+U16 = mybir.dt.uint16
+U8 = mybir.dt.uint8
+FP8X4 = mybir.dt.float8_e4m3fn_x4
+FP4X4 = mybir.dt.float4_e2m1fn_x4
+MULT = mybir.AluOpType.mult
+SIGMOID = mybir.ActivationFunctionType.Sigmoid
+
+
+def tile_list_sigS_kernel(
+    tc, xT, wgt, wk_words, wk_scales, wv_words, wv_scales, st, wgo, offs, offs2, out
+):
+    nc = tc.nc
+    with ExitStack() as ctx:
+        held = ctx.enter_context(tc.tile_pool(name="held", bufs=1))
+        ring = ctx.enter_context(tc.tile_pool(name="ring", bufs=4))
+        psum = ctx.enter_context(tc.psum_pool(name="psum", bufs=4))
+
+        picks = held.tile([P, J // 16], U16, name="picks")
+        places = held.tile([P, J // 16], U16, name="places")
+        wgt_sb = held.tile([P, J], F32, name="wgt_sb")
+        wgo_sb = held.tile([P, J], F32, name="wgo_sb")
+        planes = [held.tile([P, T], F32, name=f"plane{i}") for i in range(PACK)]
+        pages = [held.tile([P, T], F32, name=f"page{b}") for b in range(BLOCKS)]
+        states = [held.tile([P, J], F32, name=f"state{b}") for b in range(BLOCKS)]
+        wk_sb = held.tile([P, N], U32, name="wk_sb", align_bytes=64)
+        wv_sb = held.tile([P, 2 * N], U8, name="wv_sb", align_bytes=64)
+        wk_sc = held.tile([P, N], U8, name="wk_sc", align_bytes=64)
+        wv_sc = held.tile([P, N], U8, name="wv_sc", align_bytes=64)
+
+        x_planes = xT.rearrange("(p i) t -> i p t", i=PACK)
+        nc.sync.dma_start(picks[:], offs)
+        nc.sync.dma_start(wgt_sb[:], wgt)
+        for i in range(PACK):
+            nc.sync.dma_start(planes[i][:], x_planes[i])
+        nc.sync.dma_start(wk_sb[:].bitcast(I32), wk_words[0].rearrange("p n t -> p (n t)").bitcast(I32))
+        nc.sync.dma_start(wv_sb[:].bitcast(I32), wv_words[0].bitcast(I32))
+        nc.sync.dma_start(states[0][:], st[0:P, :])
+        nc.sync.dma_start(wgo_sb[:], wgo)
+        nc.sync.dma_start(places[:], offs2)
+        for b in range(1, BLOCKS):
+            nc.sync.dma_start(states[b][:], st[b * P : (b + 1) * P, :])
+
+        for plane_sc, scales in ((wk_sc, wk_scales), (wv_sc, wv_scales)):
+            nc.gpsimd.memset(plane_sc[:].bitcast(I32), 0)
+            for q in range(4):
+                nc.gpsimd.dma_start(
+                    plane_sc[32 * q : 32 * q + 4, :].bitcast(I32),
+                    scales[0, 4 * q : 4 * q + 4, :].bitcast(I32),
+                )
+
+        for b in range(BLOCKS):
+            nc.vector.memset(pages[b][:], 0.0)
+
+        picked = [held.tile([P, PACK, hi - lo], F32, name=f"picked{lo}") for lo, hi in CHUNKS]
+        for i in range(PACK):
+            for c, (lo, hi) in enumerate(CHUNKS):
+                nc.vector.tensor_tensor(
+                    picked[c][:, i, :],
+                    planes[i][:].indirect(picks[:, lo // 16 : hi // 16]),
+                    wgt_sb[:, lo:hi],
+                    MULT,
+                )
+
+        for c, (lo, hi) in enumerate(CHUNKS):
+            width = hi - lo
+            grouped = held.tile([P, width, PACK], BF16, name=f"grouped{lo}", align_bytes=64)
+            nc.scalar.copy(
+                grouped[:].rearrange("p (c i) t -> p c t i", i=4),
+                picked[c][:].rearrange("p t (c i) -> p c t i", i=4),
+            )
+            codes = held.tile([P, width], U32, name=f"codes{lo}", align_bytes=64)
+            scales = held.tile([P, width], U8, name=f"scales{lo}", align_bytes=64)
+            nc.vector.quantize_mx(
+                out=codes[:].bitcast(FP8X4),
+                scales=scales[:],
+                in_=grouped[:].rearrange("p j t -> p (j t)"),
+            )
+            for b in range(BLOCKS):
+                rows = slice(b * P, (b + 1) * P)
+                keys = psum.tile([P, 512], F32, name="keys")
+                values = psum.tile([P, 512], F32, name="values")
+                nc.tensor.matmul_mx(
+                    out=keys[:, :width],
+                    lhsT=wk_sb[:, rows].bitcast(FP8X4),
+                    lhsT_scale=wk_sc[:, rows],
+                    rhs=codes[:].bitcast(FP8X4),
+                    rhs_scale=scales[:],
+                    start=True,
+                    stop=True,
+                )
+                nc.tensor.matmul_mx(
+                    out=values[:, :width],
+                    lhsT=wv_sb[:, 2 * b * P : 2 * (b + 1) * P].bitcast(FP4X4),
+                    lhsT_scale=wv_sc[:, rows],
+                    rhs=codes[:].bitcast(FP8X4),
+                    rhs_scale=scales[:],
+                    start=True,
+                    stop=True,
+                )
+                score = ring.tile([P, 512], F32, name="score")
+                nc.vector.tensor_tensor(score[:, :width], keys[:, :width], states[b][:, lo:hi], MULT)
+                gate = ring.tile([P, 512], F32, name="gate")
+                nc.scalar.activation(gate[:, :width], score[:, :width], SIGMOID)
+                gated = ring.tile([P, 512], F32, name="gated")
+                nc.vector.tensor_tensor(gated[:, :width], values[:, :width], gate[:, :width], MULT)
+                nc.vector.tensor_tensor(
+                    pages[b][:].indirect(places[:, lo // 16 : hi // 16]),
+                    gated[:, :width],
+                    wgo_sb[:, lo:hi],
+                    MULT,
+                )
+                if hi == J:
+                    nc.sync.dma_start(out[rows, :], pages[b][:])

@@ -36,45 +36,42 @@ def tile_list_sigS_kernel(
         wgo_sb = held.tile([P, J], F32, name="wgo_sb")
         planes = [held.tile([P, T], F32, name=f"plane{i}") for i in range(PACK)]
         pages = [held.tile([P, T], F32, name=f"page{b}") for b in range(BLOCKS)]
-        states = [held.tile([P, J], F32, name=f"state{b}") for b in range(BLOCKS)]
+        states = [held.tile([P, BLOCKS, hi - lo], F32, name=f"state{lo}") for lo, hi in CHUNKS]
         wk_sb = held.tile([P, N], U32, name="wk_sb", align_bytes=64)
         wv_sb = held.tile([P, 2 * N], U8, name="wv_sb", align_bytes=64)
         wk_sc = held.tile([P, N], U8, name="wk_sc", align_bytes=64)
         wv_sc = held.tile([P, N], U8, name="wv_sc", align_bytes=64)
 
+        for plane_sc, scales in ((wk_sc, wk_scales), (wv_sc, wv_scales)):
+            nc.vector.memset(plane_sc[:].bitcast(I32), 0)
+            for q in range(4):
+                nc.scalar.dma_start(
+                    plane_sc[32 * q : 32 * q + 4, :].bitcast(I32),
+                    scales[0, 4 * q : 4 * q + 4, :].bitcast(I32),
+                )
+
         x_planes = xT.rearrange("(p i) t -> i p t", i=PACK)
+        st_blocks = st.rearrange("(b p) j -> p b j", p=P)
         nc.sync.dma_start(picks[:], offs)
         nc.sync.dma_start(wgt_sb[:], wgt)
         for i in range(PACK):
             nc.sync.dma_start(planes[i][:], x_planes[i])
         nc.sync.dma_start(wk_sb[:].bitcast(I32), wk_words[0].rearrange("p n t -> p (n t)").bitcast(I32))
         nc.sync.dma_start(wv_sb[:].bitcast(I32), wv_words[0].bitcast(I32))
-        nc.sync.dma_start(states[0][:], st[0:P, :])
+        nc.sync.dma_start(states[0][:], st_blocks[:, :, CHUNKS[0][0] : CHUNKS[0][1]])
         nc.sync.dma_start(wgo_sb[:], wgo)
         nc.sync.dma_start(places[:], offs2)
-        for b in range(1, BLOCKS):
-            nc.sync.dma_start(states[b][:], st[b * P : (b + 1) * P, :])
-
-        for plane_sc, scales in ((wk_sc, wk_scales), (wv_sc, wv_scales)):
-            nc.gpsimd.memset(plane_sc[:].bitcast(I32), 0)
-            for q in range(4):
-                nc.gpsimd.dma_start(
-                    plane_sc[32 * q : 32 * q + 4, :].bitcast(I32),
-                    scales[0, 4 * q : 4 * q + 4, :].bitcast(I32),
-                )
+        for c in range(1, len(CHUNKS)):
+            nc.sync.dma_start(states[c][:], st_blocks[:, :, CHUNKS[c][0] : CHUNKS[c][1]])
 
         for b in range(BLOCKS):
-            nc.vector.memset(pages[b][:], 0.0)
+            (nc.vector if b < 2 else nc.gpsimd).memset(pages[b][:], 0.0)
 
         picked = [held.tile([P, PACK, hi - lo], F32, name=f"picked{lo}") for lo, hi in CHUNKS]
         for i in range(PACK):
             for c, (lo, hi) in enumerate(CHUNKS):
-                nc.vector.tensor_tensor(
-                    picked[c][:, i, :],
-                    planes[i][:].indirect(picks[:, lo // 16 : hi // 16]),
-                    wgt_sb[:, lo:hi],
-                    MULT,
-                )
+                window = planes[i][:].indirect(picks[:, lo // 16 : hi // 16])
+                nc.vector.tensor_tensor(picked[c][:, i, :], window, wgt_sb[:, lo:hi], MULT)
 
         for c, (lo, hi) in enumerate(CHUNKS):
             width = hi - lo
@@ -113,16 +110,15 @@ def tile_list_sigS_kernel(
                     stop=True,
                 )
                 score = ring.tile([P, 512], F32, name="score")
-                nc.vector.tensor_tensor(score[:, :width], keys[:, :width], states[b][:, lo:hi], MULT)
+                nc.vector.tensor_tensor(score[:, :width], keys[:, :width], states[c][:, b, :], MULT)
+                values_sb = ring.tile([P, 512], F32, name="values_sb")
+                nc.scalar.copy(values_sb[:, :width], values[:, :width])
                 gate = ring.tile([P, 512], F32, name="gate")
                 nc.scalar.activation(gate[:, :width], score[:, :width], SIGMOID)
+                weighted = ring.tile([P, 512], F32, name="weighted")
+                nc.gpsimd.tensor_tensor(weighted[:, :width], values_sb[:, :width], wgo_sb[:, lo:hi], MULT)
                 gated = ring.tile([P, 512], F32, name="gated")
-                nc.vector.tensor_tensor(gated[:, :width], values[:, :width], gate[:, :width], MULT)
-                nc.vector.tensor_tensor(
-                    pages[b][:].indirect(places[:, lo // 16 : hi // 16]),
-                    gated[:, :width],
-                    wgo_sb[:, lo:hi],
-                    MULT,
-                )
+                nc.gpsimd.tensor_tensor(gated[:, :width], weighted[:, :width], gate[:, :width], MULT)
+                nc.vector.tensor_copy(pages[b][:].indirect(places[:, lo // 16 : hi // 16]), gated[:, :width])
                 if hi == J:
                     nc.sync.dma_start(out[rows, :], pages[b][:])

@@ -6,7 +6,11 @@ K, N, T, J = 512, 512, 2048, 1024
 P = 128
 PACK = 4
 BLOCKS = N // P
-CHUNKS = ((0, 256), (256, 512), (512, 1024))
+BANK = 512
+CHUNKS = ((0, 256, 1), (256, 512, 2), (512, 1024, 1))
+WEAVE = 128
+SCORE_ON_GPSIMD_FROM = 8
+EARLY = 384
 FLOPS = 2 * 2 * K * N * J
 
 F32 = mybir.dt.float32
@@ -27,7 +31,8 @@ def tile_list_sigS_kernel(
     nc = tc.nc
     with ExitStack() as ctx:
         held = ctx.enter_context(tc.tile_pool(name="held", bufs=1))
-        ring = ctx.enter_context(tc.tile_pool(name="ring", bufs=4))
+        ring = ctx.enter_context(tc.tile_pool(name="ring", bufs=6))
+        pair = ctx.enter_context(tc.tile_pool(name="pair", bufs=2))
         psum = ctx.enter_context(tc.psum_pool(name="psum", bufs=4))
 
         picks = held.tile([P, J // 16], U16, name="picks")
@@ -36,16 +41,15 @@ def tile_list_sigS_kernel(
         wgo_sb = held.tile([P, J], F32, name="wgo_sb")
         planes = [held.tile([P, T], F32, name=f"plane{i}") for i in range(PACK)]
         pages = [held.tile([P, T], F32, name=f"page{b}") for b in range(BLOCKS)]
-        states = [held.tile([P, BLOCKS, hi - lo], F32, name=f"state{lo}") for lo, hi in CHUNKS]
+        states = [held.tile([P, BLOCKS, hi - lo], F32, name=f"state{lo}") for lo, hi, group in CHUNKS]
         wk_sb = held.tile([P, N], U32, name="wk_sb", align_bytes=64)
         wv_sb = held.tile([P, 2 * N], U8, name="wv_sb", align_bytes=64)
         wk_sc = held.tile([P, N], U8, name="wk_sc", align_bytes=64)
         wv_sc = held.tile([P, N], U8, name="wv_sc", align_bytes=64)
 
-        for plane_sc, scales in ((wk_sc, wk_scales), (wv_sc, wv_scales)):
-            nc.vector.memset(plane_sc[:].bitcast(I32), 0)
+        for plane_sc, scales, queue in ((wk_sc, wk_scales, nc.scalar), (wv_sc, wv_scales, nc.gpsimd)):
             for q in range(4):
-                nc.scalar.dma_start(
+                queue.dma_start(
                     plane_sc[32 * q : 32 * q + 4, :].bitcast(I32),
                     scales[0, 4 * q : 4 * q + 4, :].bitcast(I32),
                 )
@@ -53,11 +57,13 @@ def tile_list_sigS_kernel(
         x_planes = xT.rearrange("(p i) t -> i p t", i=PACK)
         st_blocks = st.rearrange("(b p) j -> p b j", p=P)
         nc.sync.dma_start(picks[:], offs)
-        nc.sync.dma_start(wgt_sb[:], wgt)
-        for i in range(PACK):
+        nc.sync.dma_start(wgt_sb[:, :EARLY], wgt[:, :EARLY])
+        nc.sync.dma_start(planes[0][:], x_planes[0])
+        nc.sync.dma_start(wgt_sb[:, EARLY:], wgt[:, EARLY:])
+        for i in range(1, PACK):
             nc.sync.dma_start(planes[i][:], x_planes[i])
-        nc.sync.dma_start(wk_sb[:].bitcast(I32), wk_words[0].rearrange("p n t -> p (n t)").bitcast(I32))
         nc.sync.dma_start(wv_sb[:].bitcast(I32), wv_words[0].bitcast(I32))
+        nc.sync.dma_start(wk_sb[:].bitcast(I32), wk_words[0].rearrange("p n t -> p (n t)").bitcast(I32))
         nc.sync.dma_start(states[0][:], st_blocks[:, :, CHUNKS[0][0] : CHUNKS[0][1]])
         nc.sync.dma_start(wgo_sb[:], wgo)
         nc.sync.dma_start(places[:], offs2)
@@ -67,58 +73,108 @@ def tile_list_sigS_kernel(
         for b in range(BLOCKS):
             (nc.vector if b < 2 else nc.gpsimd).memset(pages[b][:], 0.0)
 
-        picked = [held.tile([P, PACK, hi - lo], F32, name=f"picked{lo}") for lo, hi in CHUNKS]
-        for i in range(PACK):
-            for c, (lo, hi) in enumerate(CHUNKS):
-                window = planes[i][:].indirect(picks[:, lo // 16 : hi // 16])
-                nc.vector.tensor_tensor(picked[c][:, i, :], window, wgt_sb[:, lo:hi], MULT)
+        picked = [held.tile([P, 2, J], F32, name=f"picked{h}") for h in range(PACK // 2)]
+        grouped = [
+            held.tile([P, hi - lo, PACK], BF16, name=f"grouped{lo}", align_bytes=64) for lo, hi, group in CHUNKS
+        ]
+        codes = [held.tile([P, hi - lo], U32, name=f"codes{lo}", align_bytes=64) for lo, hi, group in CHUNKS]
+        code_sc = [held.tile([P, hi - lo], U8, name=f"code_sc{lo}", align_bytes=64) for lo, hi, group in CHUNKS]
 
-        for c, (lo, hi) in enumerate(CHUNKS):
-            width = hi - lo
-            grouped = held.tile([P, width, PACK], BF16, name=f"grouped{lo}", align_bytes=64)
-            nc.scalar.copy(
-                grouped[:].rearrange("p (c i) t -> p c t i", i=4),
-                picked[c][:].rearrange("p t (c i) -> p c t i", i=4),
-            )
-            codes = held.tile([P, width], U32, name=f"codes{lo}", align_bytes=64)
-            scales = held.tile([P, width], U8, name=f"scales{lo}", align_bytes=64)
+        def gather(i, lo, hi):
+            window = planes[i][:].indirect(picks[:, lo // 16 : hi // 16])
+            nc.vector.tensor_tensor(picked[i // 2][:, i % 2, lo:hi], window, wgt_sb[:, lo:hi], MULT)
+
+        def weave(c, i0):
+            lo, hi, group = CHUNKS[c]
+            piece = min(WEAVE, hi - lo)
+            for j0 in range(0, hi - lo, piece):
+                nc.scalar.copy(
+                    grouped[c][:, j0 : j0 + piece, i0 : i0 + 2].rearrange("p (c i) t -> p c i t", i=4),
+                    picked[i0 // 2][:, :, lo + j0 : lo + j0 + piece].rearrange("p t (c i) -> p c i t", i=4),
+                )
+
+        def quantize(c):
             nc.vector.quantize_mx(
-                out=codes[:].bitcast(FP8X4),
-                scales=scales[:],
-                in_=grouped[:].rearrange("p j t -> p (j t)"),
+                out=codes[c][:].bitcast(FP8X4),
+                scales=code_sc[c][:],
+                in_=grouped[c][:].rearrange("p j t -> p (j t)"),
             )
-            for b in range(BLOCKS):
-                rows = slice(b * P, (b + 1) * P)
-                keys = psum.tile([P, 512], F32, name="keys")
-                values = psum.tile([P, 512], F32, name="values")
+
+        def step(c, b0, score_on_gpsimd):
+            lo, hi, group = CHUNKS[c]
+            width = hi - lo
+            span = group * width
+            keys = psum.tile([P, BANK], F32, name="keys")
+            values = psum.tile([P, BANK], F32, name="values")
+            for g in range(group):
+                rows = slice((b0 + g) * P, (b0 + g + 1) * P)
                 nc.tensor.matmul_mx(
-                    out=keys[:, :width],
+                    out=values[:, g * width : (g + 1) * width],
+                    lhsT=wv_sb[:, 2 * rows.start : 2 * rows.stop].bitcast(FP4X4),
+                    lhsT_scale=wv_sc[:, rows],
+                    rhs=codes[c][:].bitcast(FP8X4),
+                    rhs_scale=code_sc[c][:],
+                    start=True,
+                    stop=True,
+                )
+            for g in range(group):
+                rows = slice((b0 + g) * P, (b0 + g + 1) * P)
+                nc.tensor.matmul_mx(
+                    out=keys[:, g * width : (g + 1) * width],
                     lhsT=wk_sb[:, rows].bitcast(FP8X4),
                     lhsT_scale=wk_sc[:, rows],
-                    rhs=codes[:].bitcast(FP8X4),
-                    rhs_scale=scales[:],
+                    rhs=codes[c][:].bitcast(FP8X4),
+                    rhs_scale=code_sc[c][:],
                     start=True,
                     stop=True,
                 )
-                nc.tensor.matmul_mx(
-                    out=values[:, :width],
-                    lhsT=wv_sb[:, 2 * b * P : 2 * (b + 1) * P].bitcast(FP4X4),
-                    lhsT_scale=wv_sc[:, rows],
-                    rhs=codes[:].bitcast(FP8X4),
-                    rhs_scale=scales[:],
-                    start=True,
-                    stop=True,
+            state = states[c][:, b0 : b0 + group, :].rearrange("p g j -> p (g j)")
+            if score_on_gpsimd:
+                score = pair.tile([P, BANK], F32, name="score_g", tag="gpsimd_out")
+                keys_sb = pair.tile([P, BANK], F32, name="keys_sb")
+                nc.scalar.copy(keys_sb[:, :span], keys[:, :span])
+                nc.gpsimd.tensor_tensor(score[:, :span], keys_sb[:, :span], state, MULT)
+            else:
+                score = ring.tile([P, BANK], F32, name="score")
+                nc.vector.tensor_tensor(score[:, :span], keys[:, :span], state, MULT)
+            values_sb = pair.tile([P, BANK], F32, name="values_sb")
+            nc.scalar.copy(values_sb[:, :span], values[:, :span])
+            gate = ring.tile([P, BANK], F32, name="gate")
+            nc.scalar.activation(gate[:, :span], score[:, :span], SIGMOID)
+            weighted = pair.tile([P, BANK], F32, name="weighted", tag="gpsimd_out")
+            nc.gpsimd.tensor_tensor(
+                weighted[:, :span].rearrange("p (g j) -> p g j", g=group),
+                values_sb[:, :span].rearrange("p (g j) -> p g j", g=group),
+                wgo_sb[:, lo:hi].rearrange("p (g j) -> p g j", g=1).to_broadcast([P, group, width]),
+                MULT,
+            )
+            gated = ring.tile([P, BANK], F32, name="gated")
+            nc.gpsimd.tensor_tensor(gated[:, :span], weighted[:, :span], gate[:, :span], MULT)
+            for g in range(group):
+                b = b0 + g
+                nc.vector.tensor_copy(
+                    pages[b][:].indirect(places[:, lo // 16 : hi // 16]),
+                    gated[:, g * width : (g + 1) * width],
                 )
-                score = ring.tile([P, 512], F32, name="score")
-                nc.vector.tensor_tensor(score[:, :width], keys[:, :width], states[c][:, b, :], MULT)
-                values_sb = ring.tile([P, 512], F32, name="values_sb")
-                nc.scalar.copy(values_sb[:, :width], values[:, :width])
-                gate = ring.tile([P, 512], F32, name="gate")
-                nc.scalar.activation(gate[:, :width], score[:, :width], SIGMOID)
-                weighted = ring.tile([P, 512], F32, name="weighted")
-                nc.gpsimd.tensor_tensor(weighted[:, :width], values_sb[:, :width], wgo_sb[:, lo:hi], MULT)
-                gated = ring.tile([P, 512], F32, name="gated")
-                nc.gpsimd.tensor_tensor(gated[:, :width], weighted[:, :width], gate[:, :width], MULT)
-                nc.vector.tensor_copy(pages[b][:].indirect(places[:, lo // 16 : hi // 16]), gated[:, :width])
                 if hi == J:
-                    nc.sync.dma_start(out[rows, :], pages[b][:])
+                    nc.sync.dma_start(out[b * P : (b + 1) * P, :], pages[b][:])
+
+        chunks = range(len(CHUNKS))
+        last = PACK - 1
+        gather(0, 0, EARLY)
+        gather(0, EARLY, J)
+        gather(1, 0, J // 2)
+        gather(1, J // 2, J)
+        for c in chunks:
+            weave(c, 0)
+        gather(2, 0, J)
+        steps = [(c, b0) for c in chunks for b0 in range(0, BLOCKS, CHUNKS[c][2])]
+        for c in chunks:
+            if c == len(CHUNKS) - 1:
+                for count in range(4):
+                    step(*steps[count], False)
+            gather(last, CHUNKS[c][0], CHUNKS[c][1])
+            weave(c, 2)
+            quantize(c)
+        for count in range(4, len(steps)):
+            step(*steps[count], count >= SCORE_ON_GPSIMD_FROM)

@@ -9,7 +9,7 @@ BLOCKS = N // P
 BANK = 512
 CHUNKS = ((0, 256, 1), (256, 512, 2), (512, 1024, 1))
 WEAVE = 128
-SCORE_ON_GPSIMD_FROM = 8
+SCORE_ON_GPSIMD_FROM = 7
 EARLY = 384
 FLOPS = 2 * 2 * K * N * J
 
@@ -47,7 +47,7 @@ def tile_list_sigS_kernel(
         wk_sc = held.tile([P, N], U8, name="wk_sc", align_bytes=64)
         wv_sc = held.tile([P, N], U8, name="wv_sc", align_bytes=64)
 
-        for plane_sc, scales, queue in ((wk_sc, wk_scales, nc.scalar), (wv_sc, wv_scales, nc.gpsimd)):
+        for plane_sc, scales, queue in ((wv_sc, wv_scales, nc.scalar), (wk_sc, wk_scales, nc.gpsimd)):
             for q in range(4):
                 queue.dma_start(
                     plane_sc[32 * q : 32 * q + 4, :].bitcast(I32),

@@ -7,10 +7,11 @@ P = 128
 PACK = 4
 BLOCKS = N // P
 BANK = 512
-CHUNKS = ((0, 256, 1), (256, 512, 2), (512, 1024, 1))
+CHUNKS = ((0, 256), (256, 512), (512, 1024))
 WEAVE = 128
-SCORE_ON_GPSIMD_FROM = 7
 EARLY = 384
+LAST = 256
+SCORE_ON_GPSIMD_FROM = 2
 FLOPS = 2 * 2 * K * N * J
 
 F32 = mybir.dt.float32
@@ -31,28 +32,34 @@ def tile_list_sigS_kernel(
     nc = tc.nc
     with ExitStack() as ctx:
         held = ctx.enter_context(tc.tile_pool(name="held", bufs=1))
-        ring = ctx.enter_context(tc.tile_pool(name="ring", bufs=6))
-        pair = ctx.enter_context(tc.tile_pool(name="pair", bufs=2))
+        turn = ctx.enter_context(tc.tile_pool(name="turn", bufs=2))
         psum = ctx.enter_context(tc.psum_pool(name="psum", bufs=4))
 
         picks = held.tile([P, J // 16], U16, name="picks")
         places = held.tile([P, J // 16], U16, name="places")
         wgt_sb = held.tile([P, J], F32, name="wgt_sb")
-        wgo_sb = held.tile([P, J], F32, name="wgo_sb")
+        wgo_sb = [held.tile([P, hi - lo], F32, name=f"wgo{lo}") for lo, hi in CHUNKS]
         planes = [held.tile([P, T], F32, name=f"plane{i}") for i in range(PACK)]
         pages = [held.tile([P, T], F32, name=f"page{b}") for b in range(BLOCKS)]
-        states = [held.tile([P, BLOCKS, hi - lo], F32, name=f"state{lo}") for lo, hi, group in CHUNKS]
+        states = [held.tile([P, BLOCKS, hi - lo], F32, name=f"state{lo}") for lo, hi in CHUNKS]
         wk_sb = held.tile([P, N], U32, name="wk_sb", align_bytes=64)
         wv_sb = held.tile([P, 2 * N], U8, name="wv_sb", align_bytes=64)
         wk_sc = held.tile([P, N], U8, name="wk_sc", align_bytes=64)
         wv_sc = held.tile([P, N], U8, name="wv_sc", align_bytes=64)
 
-        for plane_sc, scales, queue in ((wv_sc, wv_scales, nc.scalar), (wk_sc, wk_scales, nc.gpsimd)):
+        def load_scales(queue, plane_sc, scales):
             for q in range(4):
                 queue.dma_start(
                     plane_sc[32 * q : 32 * q + 4, :].bitcast(I32),
                     scales[0, 4 * q : 4 * q + 4, :].bitcast(I32),
                 )
+
+        load_scales(nc.scalar, wv_sc, wv_scales)
+        load_scales(nc.gpsimd, wk_sc, wk_scales)
+
+        warm = held.tile([P, 1], F32, name="warm")
+        nc.gpsimd.memset(warm[:], 0.0)
+        nc.scalar.activation(warm[:], warm[:], SIGMOID)
 
         x_planes = xT.rearrange("(p i) t -> i p t", i=PACK)
         st_blocks = st.rearrange("(b p) j -> p b j", p=P)
@@ -64,103 +71,103 @@ def tile_list_sigS_kernel(
             nc.sync.dma_start(planes[i][:], x_planes[i])
         nc.sync.dma_start(wv_sb[:].bitcast(I32), wv_words[0].bitcast(I32))
         nc.sync.dma_start(wk_sb[:].bitcast(I32), wk_words[0].rearrange("p n t -> p (n t)").bitcast(I32))
-        nc.sync.dma_start(states[0][:], st_blocks[:, :, CHUNKS[0][0] : CHUNKS[0][1]])
-        nc.sync.dma_start(wgo_sb[:], wgo)
-        nc.sync.dma_start(places[:], offs2)
-        for c in range(1, len(CHUNKS)):
-            nc.sync.dma_start(states[c][:], st_blocks[:, :, CHUNKS[c][0] : CHUNKS[c][1]])
+        for c, (lo, hi) in enumerate(CHUNKS):
+            nc.sync.dma_start(states[c][:], st_blocks[:, :, lo:hi])
+            nc.sync.dma_start(wgo_sb[c][:], wgo[:, lo:hi])
+            if c == 0:
+                nc.sync.dma_start(places[:], offs2)
 
         for b in range(BLOCKS):
-            (nc.vector if b < 2 else nc.gpsimd).memset(pages[b][:], 0.0)
+            nc.gpsimd.memset(pages[b][:], 0.0)
 
-        picked = [held.tile([P, 2, J], F32, name=f"picked{h}") for h in range(PACK // 2)]
-        grouped = [
-            held.tile([P, hi - lo, PACK], BF16, name=f"grouped{lo}", align_bytes=64) for lo, hi, group in CHUNKS
+        picked = [held.tile([P, 2, J], F32, name=f"picked{h}", align_bytes=64) for h in range(PACK // 2)]
+        first = picked[1][:, 1, CHUNKS[-1][0] : J].bitcast(BF16).rearrange("p (j t) -> p j t", t=PACK)
+        grouped = [first] + [
+            held.tile([P, hi - lo, PACK], BF16, name=f"grouped{lo}", align_bytes=64)[:] for lo, hi in CHUNKS[1:]
         ]
-        codes = [held.tile([P, hi - lo], U32, name=f"codes{lo}", align_bytes=64) for lo, hi, group in CHUNKS]
-        code_sc = [held.tile([P, hi - lo], U8, name=f"code_sc{lo}", align_bytes=64) for lo, hi, group in CHUNKS]
+        codes = [held.tile([P, hi - lo], U32, name=f"codes{lo}", align_bytes=64) for lo, hi in CHUNKS]
+        code_sc = [held.tile([P, hi - lo], U8, name=f"code_sc{lo}", align_bytes=64) for lo, hi in CHUNKS]
 
         def gather(i, lo, hi):
             window = planes[i][:].indirect(picks[:, lo // 16 : hi // 16])
             nc.vector.tensor_tensor(picked[i // 2][:, i % 2, lo:hi], window, wgt_sb[:, lo:hi], MULT)
 
         def weave(c, i0):
-            lo, hi, group = CHUNKS[c]
-            piece = min(WEAVE, hi - lo)
-            for j0 in range(0, hi - lo, piece):
+            lo, hi = CHUNKS[c]
+            for j0 in range(0, hi - lo, WEAVE):
                 nc.scalar.copy(
-                    grouped[c][:, j0 : j0 + piece, i0 : i0 + 2].rearrange("p (c i) t -> p c i t", i=4),
-                    picked[i0 // 2][:, :, lo + j0 : lo + j0 + piece].rearrange("p t (c i) -> p c i t", i=4),
+                    grouped[c][:, j0 : j0 + WEAVE, i0 : i0 + 2].rearrange("p (c i) t -> p c i t", i=4),
+                    picked[i0 // 2][:, :, lo + j0 : lo + j0 + WEAVE].rearrange("p t (c i) -> p c i t", i=4),
                 )
 
         def quantize(c):
             nc.vector.quantize_mx(
                 out=codes[c][:].bitcast(FP8X4),
                 scales=code_sc[c][:],
-                in_=grouped[c][:].rearrange("p j t -> p (j t)"),
+                in_=grouped[c].rearrange("p j t -> p (j t)"),
             )
 
-        def step(c, b0, score_on_gpsimd):
-            lo, hi, group = CHUNKS[c]
+        def multiply(c, b0):
+            lo, hi = CHUNKS[c]
             width = hi - lo
-            span = group * width
             keys = psum.tile([P, BANK], F32, name="keys")
             values = psum.tile([P, BANK], F32, name="values")
-            for g in range(group):
-                rows = slice((b0 + g) * P, (b0 + g + 1) * P)
-                nc.tensor.matmul_mx(
-                    out=values[:, g * width : (g + 1) * width],
-                    lhsT=wv_sb[:, 2 * rows.start : 2 * rows.stop].bitcast(FP4X4),
-                    lhsT_scale=wv_sc[:, rows],
-                    rhs=codes[c][:].bitcast(FP8X4),
-                    rhs_scale=code_sc[c][:],
-                    start=True,
-                    stop=True,
-                )
-            for g in range(group):
-                rows = slice((b0 + g) * P, (b0 + g + 1) * P)
-                nc.tensor.matmul_mx(
-                    out=keys[:, g * width : (g + 1) * width],
-                    lhsT=wk_sb[:, rows].bitcast(FP8X4),
-                    lhsT_scale=wk_sc[:, rows],
-                    rhs=codes[c][:].bitcast(FP8X4),
-                    rhs_scale=code_sc[c][:],
-                    start=True,
-                    stop=True,
-                )
-            state = states[c][:, b0 : b0 + group, :].rearrange("p g j -> p (g j)")
-            if score_on_gpsimd:
-                score = pair.tile([P, BANK], F32, name="score_g", tag="gpsimd_out")
-                keys_sb = pair.tile([P, BANK], F32, name="keys_sb")
-                nc.scalar.copy(keys_sb[:, :span], keys[:, :span])
-                nc.gpsimd.tensor_tensor(score[:, :span], keys_sb[:, :span], state, MULT)
+            for bank, words, scales, size, view in ((values, wv_sb, wv_sc, 2, FP4X4), (keys, wk_sb, wk_sc, 1, FP8X4)):
+                for g in range(BANK // width):
+                    rows = slice((b0 + g) * P, (b0 + g + 1) * P)
+                    nc.tensor.matmul_mx(
+                        out=bank[:, g * width : (g + 1) * width],
+                        lhsT=words[:, size * rows.start : size * rows.stop].bitcast(view),
+                        lhsT_scale=scales[:, rows],
+                        rhs=codes[c][:].bitcast(FP8X4),
+                        rhs_scale=code_sc[c][:],
+                        start=True,
+                        stop=True,
+                    )
+            return keys, values
+
+        def score(c, b0, group, j0, width, keys):
+            span = group * width
+            name = f"{b0}_{CHUNKS[c][0] + j0}"
+            state = states[c][:, b0 : b0 + group, j0 : j0 + width].rearrange("p g j -> p (g j)")
+            if c >= SCORE_ON_GPSIMD_FROM:
+                keys_sb = held.tile([P, span], F32, name=f"keys{name}")
+                gate = turn.tile([P, span], F32, name="gate")
+                nc.scalar.copy(keys_sb[:], keys)
+                nc.gpsimd.tensor_tensor(gate[:], keys_sb[:], state, MULT)
             else:
-                score = ring.tile([P, BANK], F32, name="score")
-                nc.vector.tensor_tensor(score[:, :span], keys[:, :span], state, MULT)
-            values_sb = pair.tile([P, BANK], F32, name="values_sb")
-            nc.scalar.copy(values_sb[:, :span], values[:, :span])
-            gate = ring.tile([P, BANK], F32, name="gate")
-            nc.scalar.activation(gate[:, :span], score[:, :span], SIGMOID)
-            weighted = pair.tile([P, BANK], F32, name="weighted", tag="gpsimd_out")
+                gate = held.tile([P, span], F32, name=f"gate{name}")
+                nc.vector.tensor_tensor(gate[:], keys, state, MULT)
+            return gate
+
+        def finish(c, b0, group, j0, width, gate, values, last, reuse=None):
+            lo = CHUNKS[c][0] + j0
+            span = group * width
+            name = f"{b0}_{lo}"
+            result = held.tile([P, span], F32, name=f"result{name}")
+            nc.scalar.copy(result[:], values)
+            nc.scalar.activation(gate[:], gate[:], SIGMOID)
+            weighted = turn.tile([P, span], F32, name="weighted")
             nc.gpsimd.tensor_tensor(
-                weighted[:, :span].rearrange("p (g j) -> p g j", g=group),
-                values_sb[:, :span].rearrange("p (g j) -> p g j", g=group),
-                wgo_sb[:, lo:hi].rearrange("p (g j) -> p g j", g=1).to_broadcast([P, group, width]),
+                weighted[:].rearrange("p (g j) -> p g j", g=group),
+                result[:].rearrange("p (g j) -> p g j", g=group),
+                wgo_sb[c][:, j0 : j0 + width].rearrange("p (g j) -> p g j", g=1).to_broadcast([P, group, width]),
                 MULT,
             )
-            gated = ring.tile([P, BANK], F32, name="gated")
-            nc.gpsimd.tensor_tensor(gated[:, :span], weighted[:, :span], gate[:, :span], MULT)
+            gated = result[:] if reuse is None else reuse
+            if not last:
+                nc.gpsimd.tensor_tensor(gated, weighted[:], gate[:], MULT)
             for g in range(group):
                 b = b0 + g
-                nc.vector.tensor_copy(
-                    pages[b][:].indirect(places[:, lo // 16 : hi // 16]),
-                    gated[:, g * width : (g + 1) * width],
-                )
-                if hi == J:
+                target = pages[b][:].indirect(places[:, lo // 16 : (lo + width) // 16])
+                if last:
+                    nc.vector.tensor_tensor(target, weighted[:], gate[:], MULT)
+                else:
+                    nc.vector.tensor_copy(target, gated[:, g * width : (g + 1) * width])
+                if lo + width == J:
                     nc.sync.dma_start(out[b * P : (b + 1) * P, :], pages[b][:])
 
         chunks = range(len(CHUNKS))
-        last = PACK - 1
         gather(0, 0, EARLY)
         gather(0, EARLY, J)
         gather(1, 0, J // 2)
@@ -168,13 +175,26 @@ def tile_list_sigS_kernel(
         for c in chunks:
             weave(c, 0)
         gather(2, 0, J)
-        steps = [(c, b0) for c in chunks for b0 in range(0, BLOCKS, CHUNKS[c][2])]
-        for c in chunks:
-            if c == len(CHUNKS) - 1:
-                for count in range(4):
-                    step(*steps[count], False)
-            gather(last, CHUNKS[c][0], CHUNKS[c][1])
+        small = CHUNKS[0][1]
+        for c in (0, 1):
+            gather(PACK - 1, *CHUNKS[c])
             weave(c, 2)
             quantize(c)
-        for count in range(4, len(steps)):
-            step(*steps[count], count >= SCORE_ON_GPSIMD_FROM)
+        banks = [multiply(c, b0) for c in (0, 1) for b0 in (0, 2)]
+        gather(PACK - 1, *CHUNKS[2])
+        early = [(0, 0, 1, 0, 0), (0, 1, 1, 0, small), (0, 2, 2, 1, 0), (1, 0, 2, 2, 0), (1, 2, 2, 3, 0)]
+        gates = [score(c, b0, group, 0, small, banks[n][0][:, at : at + group * small]) for c, b0, group, n, at in early]
+        after_quantize = grouped[2].rearrange("p j t -> p (j t)").bitcast(F32)[:, :BANK]
+        for count, (c, b0, group, n, at) in enumerate(early):
+            values = banks[n][1][:, at : at + group * small]
+            finish(c, b0, group, 0, small, gates[count], values, False, after_quantize if count == 2 else None)
+            if count == 1:
+                weave(2, 2)
+                quantize(2)
+        for b0 in range(BLOCKS):
+            keys, values = multiply(2, b0)
+            width = BANK if b0 < BLOCKS - 1 else LAST
+            for j0 in range(0, BANK, width):
+                cols = slice(j0, j0 + width)
+                gate = score(2, b0, 1, j0, width, keys[:, cols])
+                finish(2, b0, 1, j0, width, gate, values[:, cols], b0 == BLOCKS - 1 and j0 + width == BANK)

@@ -1,17 +1,19 @@
 from contextlib import ExitStack
 
 import concourse.mybir as mybir
+from concourse.masks import make_identity
 
 K, N, T, J = 512, 512, 2048, 1024
 P = 128
 PACK = 4
 BLOCKS = N // P
+GROUPS = 8
+GROUP = P // GROUPS
 BANK = 512
 CHUNKS = ((0, 256), (256, 512), (512, 1024))
 WEAVE = 128
 EARLY = 384
 LAST = 256
-SCORE_ON_GPSIMD_FROM = 2
 FLOPS = 2 * 2 * K * N * J
 
 F32 = mybir.dt.float32
@@ -24,6 +26,7 @@ FP8X4 = mybir.dt.float8_e4m3fn_x4
 FP4X4 = mybir.dt.float4_e2m1fn_x4
 MULT = mybir.AluOpType.mult
 SIGMOID = mybir.ActivationFunctionType.Sigmoid
+COPY = mybir.ActivationFunctionType.Copy
 
 
 def tile_list_sigS_kernel(
@@ -32,13 +35,17 @@ def tile_list_sigS_kernel(
     nc = tc.nc
     with ExitStack() as ctx:
         held = ctx.enter_context(tc.tile_pool(name="held", bufs=1))
-        turn = ctx.enter_context(tc.tile_pool(name="turn", bufs=2))
-        psum = ctx.enter_context(tc.psum_pool(name="psum", bufs=4))
+        psum = ctx.enter_context(tc.psum_pool(name="psum", bufs=3))
+        psum_t = ctx.enter_context(tc.psum_pool(name="psum_t", bufs=2))
 
+        small = CHUNKS[0][1]
         picks = held.tile([P, J // 16], U16, name="picks")
         places = held.tile([P, J // 16], U16, name="places")
         wgt_sb = held.tile([P, J], F32, name="wgt_sb")
-        wgo_sb = [held.tile([P, hi - lo], F32, name=f"wgo{lo}") for lo, hi in CHUNKS]
+        wgo_first = [held.tile([P, small], F32, name=f"wgo_first{c}") for c in (0, 1)]
+        wgo_rows = held.tile([P, P], F32, name="wgo_rows")
+        wgo_t = held.tile([P, P], F32, name="wgo_t")
+        identity = held.tile([P, P], F32, name="identity")
         planes = [held.tile([P, T], F32, name=f"plane{i}") for i in range(PACK)]
         pages = [held.tile([P, T], F32, name=f"page{b}") for b in range(BLOCKS)]
         states = [held.tile([P, BLOCKS, hi - lo], F32, name=f"state{lo}") for lo, hi in CHUNKS]
@@ -47,18 +54,15 @@ def tile_list_sigS_kernel(
         wk_sc = held.tile([P, N], U8, name="wk_sc", align_bytes=64)
         wv_sc = held.tile([P, N], U8, name="wv_sc", align_bytes=64)
 
-        def load_scales(queue, plane_sc, scales):
+        for plane_sc, scales, queue in ((wv_sc, wv_scales, nc.scalar), (wk_sc, wk_scales, nc.gpsimd)):
             for q in range(4):
                 queue.dma_start(
                     plane_sc[32 * q : 32 * q + 4, :].bitcast(I32),
                     scales[0, 4 * q : 4 * q + 4, :].bitcast(I32),
                 )
 
-        load_scales(nc.scalar, wv_sc, wv_scales)
-        load_scales(nc.gpsimd, wk_sc, wk_scales)
-
         warm = held.tile([P, 1], F32, name="warm")
-        nc.gpsimd.memset(warm[:], 0.0)
+        nc.vector.memset(warm[:], 0.0)
         nc.scalar.activation(warm[:], warm[:], SIGMOID)
 
         x_planes = xT.rearrange("(p i) t -> i p t", i=PACK)
@@ -67,134 +71,189 @@ def tile_list_sigS_kernel(
         nc.sync.dma_start(wgt_sb[:, :EARLY], wgt[:, :EARLY])
         nc.sync.dma_start(planes[0][:], x_planes[0])
         nc.sync.dma_start(wgt_sb[:, EARLY:], wgt[:, EARLY:])
-        for i in range(1, PACK):
+        nc.sync.dma_start(planes[1][:], x_planes[1])
+        nc.sync.dma_start(wgo_rows[:], wgo.rearrange("(h r) (u j) -> r h u j", r=8, j=P)[0])
+        for i in range(2, PACK):
             nc.sync.dma_start(planes[i][:], x_planes[i])
         nc.sync.dma_start(wv_sb[:].bitcast(I32), wv_words[0].bitcast(I32))
         nc.sync.dma_start(wk_sb[:].bitcast(I32), wk_words[0].rearrange("p n t -> p (n t)").bitcast(I32))
-        for c, (lo, hi) in enumerate(CHUNKS):
-            nc.sync.dma_start(states[c][:], st_blocks[:, :, lo:hi])
-            nc.sync.dma_start(wgo_sb[c][:], wgo[:, lo:hi])
-            if c == 0:
-                nc.sync.dma_start(places[:], offs2)
+        nc.sync.dma_start(states[0][:], st_blocks[:, :, :small])
+        nc.sync.dma_start(wgo_first[0][:], wgo[:, :small])
+        nc.sync.dma_start(places[:], offs2)
+        nc.sync.dma_start(states[1][:], st_blocks[:, :, small : 2 * small])
+        nc.sync.dma_start(wgo_first[1][:], wgo[:, small : 2 * small])
+        nc.sync.dma_start(states[2][:], st_blocks[:, :, 2 * small :])
 
+        make_identity(nc, identity[:])
         for b in range(BLOCKS):
-            nc.gpsimd.memset(pages[b][:], 0.0)
+            (nc.vector if b < 2 else nc.gpsimd).memset(pages[b][:], 0.0)
+        turned = psum.tile([P, BANK], F32, name="rows")
+        nc.tensor.transpose(turned[:, :P], wgo_rows[:], identity[:])
+        nc.scalar.copy(wgo_t[:], turned[:, :P])
 
         picked = [held.tile([P, 2, J], F32, name=f"picked{h}", align_bytes=64) for h in range(PACK // 2)]
-        first = picked[1][:, 1, CHUNKS[-1][0] : J].bitcast(BF16).rearrange("p (j t) -> p j t", t=PACK)
-        grouped = [first] + [
-            held.tile([P, hi - lo, PACK], BF16, name=f"grouped{lo}", align_bytes=64)[:] for lo, hi in CHUNKS[1:]
-        ]
+        grouped = [held.tile([P, small, PACK], BF16, name=f"grouped{q}", align_bytes=64) for q in range(J // small)]
         codes = [held.tile([P, hi - lo], U32, name=f"codes{lo}", align_bytes=64) for lo, hi in CHUNKS]
         code_sc = [held.tile([P, hi - lo], U8, name=f"code_sc{lo}", align_bytes=64) for lo, hi in CHUNKS]
+        gates = held.tile([P, 4 * BANK], F32, name="gates")
 
         def gather(i, lo, hi):
             window = planes[i][:].indirect(picks[:, lo // 16 : hi // 16])
             nc.vector.tensor_tensor(picked[i // 2][:, i % 2, lo:hi], window, wgt_sb[:, lo:hi], MULT)
 
-        def weave(c, i0):
-            lo, hi = CHUNKS[c]
-            for j0 in range(0, hi - lo, WEAVE):
+        def weave(q, i0):
+            for j0 in range(0, small, WEAVE):
                 nc.scalar.copy(
-                    grouped[c][:, j0 : j0 + WEAVE, i0 : i0 + 2].rearrange("p (c i) t -> p c i t", i=4),
-                    picked[i0 // 2][:, :, lo + j0 : lo + j0 + WEAVE].rearrange("p t (c i) -> p c i t", i=4),
+                    grouped[q][:, j0 : j0 + WEAVE, i0 : i0 + 2].rearrange("p (c i) t -> p c i t", i=4),
+                    picked[i0 // 2][:, :, q * small + j0 : q * small + j0 + WEAVE].rearrange("p t (c i) -> p c i t", i=4),
                 )
 
-        def quantize(c):
+        def quantize(q):
+            c = min(q, 2)
+            cols = slice(q * small - CHUNKS[c][0], (q + 1) * small - CHUNKS[c][0])
             nc.vector.quantize_mx(
-                out=codes[c][:].bitcast(FP8X4),
-                scales=code_sc[c][:],
-                in_=grouped[c].rearrange("p j t -> p (j t)"),
+                out=codes[c][:, cols].bitcast(FP8X4),
+                scales=code_sc[c][:, cols],
+                in_=grouped[q][:].rearrange("p j t -> p (j t)"),
             )
 
-        def multiply(c, b0):
+        def multiply(c, b0, name, words, scales, size, view):
+            width = CHUNKS[c][1] - CHUNKS[c][0]
+            bank = psum.tile([P, BANK], F32, name=name)
+            for g in range(BANK // width):
+                rows = slice((b0 + g) * P, (b0 + g + 1) * P)
+                nc.tensor.matmul_mx(
+                    out=bank[:, g * width : (g + 1) * width],
+                    lhsT=words[:, size * rows.start : size * rows.stop].bitcast(view),
+                    lhsT_scale=scales[:, rows],
+                    rhs=codes[c][:].bitcast(FP8X4),
+                    rhs_scale=code_sc[c][:],
+                    start=True,
+                    stop=True,
+                )
+            return bank
+
+        def keys_of(c, b0):
+            return multiply(c, b0, "keys", wk_sb, wk_sc, 1, FP8X4)
+
+        def weighted_t(c):
             lo, hi = CHUNKS[c]
-            width = hi - lo
-            keys = psum.tile([P, BANK], F32, name="keys")
-            values = psum.tile([P, BANK], F32, name="values")
-            for bank, words, scales, size, view in ((values, wv_sb, wv_sc, 2, FP4X4), (keys, wk_sb, wk_sc, 1, FP8X4)):
-                for g in range(BANK // width):
-                    rows = slice((b0 + g) * P, (b0 + g + 1) * P)
-                    nc.tensor.matmul_mx(
-                        out=bank[:, g * width : (g + 1) * width],
-                        lhsT=words[:, size * rows.start : size * rows.stop].bitcast(view),
-                        lhsT_scale=scales[:, rows],
-                        rhs=codes[c][:].bitcast(FP8X4),
-                        rhs_scale=code_sc[c][:],
-                        start=True,
-                        stop=True,
+            scaled = held.tile([P, (hi - lo) // P, N], F32, name=f"scaled{lo}")
+            for u in range((hi - lo) // P):
+                entries = slice(u * P, (u + 1) * P)
+                bank = psum_t.tile([P, N], F32, name="values_t")
+                nc.tensor.matmul_mx(
+                    out=bank[:],
+                    lhsT=codes[c][:, entries].bitcast(FP8X4),
+                    lhsT_scale=code_sc[c][:, entries],
+                    rhs=wv_sb[:].bitcast(FP4X4),
+                    rhs_scale=wv_sc[:],
+                    start=True,
+                    stop=True,
+                )
+                for g in range(GROUPS):
+                    rows = slice(g * GROUP, (g + 1) * GROUP)
+                    column = 2 * g * (J // P) + lo // P + u
+                    nc.scalar.activation(
+                        scaled[:, u, :].rearrange("p (b r) -> p b r", r=P)[:, :, rows],
+                        bank[:].rearrange("p (b r) -> p b r", r=P)[:, :, rows],
+                        COPY,
+                        scale=wgo_t[:, column : column + 1],
                     )
-            return keys, values
+            return scaled
 
-        def score(c, b0, group, j0, width, keys):
-            span = group * width
-            name = f"{b0}_{CHUNKS[c][0] + j0}"
-            state = states[c][:, b0 : b0 + group, j0 : j0 + width].rearrange("p g j -> p (g j)")
-            if c >= SCORE_ON_GPSIMD_FROM:
-                keys_sb = held.tile([P, span], F32, name=f"keys{name}")
-                gate = turn.tile([P, span], F32, name="gate")
-                nc.scalar.copy(keys_sb[:], keys)
-                nc.gpsimd.tensor_tensor(gate[:], keys_sb[:], state, MULT)
-            else:
-                gate = held.tile([P, span], F32, name=f"gate{name}")
-                nc.vector.tensor_tensor(gate[:], keys, state, MULT)
-            return gate
+        def turn_back(scaled, b0, group):
+            tiles = scaled.shape[1]
+            bank = psum.tile([P, BANK], F32, name="rows")
+            for g in range(group):
+                for u in range(tiles):
+                    at = (g * tiles + u) * P
+                    nc.tensor.transpose(
+                        bank[:, at : at + P], scaled[:, u, (b0 + g) * P : (b0 + g + 1) * P], identity[:]
+                    )
+            return bank
 
-        def finish(c, b0, group, j0, width, gate, values, last, reuse=None):
+        def out_of_psum(bank, name):
+            landed = held.tile([P, bank.shape[1]], F32, name=name)
+            nc.scalar.copy(landed[:], bank)
+            return landed
+
+        def state_of(c, b0, group, j0, width):
+            return states[c][:, b0 : b0 + group, j0 : j0 + width].rearrange("p g j -> p (g j)")
+
+        def finish(c, b0, group, j0, width, gate, weighted, gated):
             lo = CHUNKS[c][0] + j0
-            span = group * width
-            name = f"{b0}_{lo}"
-            result = held.tile([P, span], F32, name=f"result{name}")
-            nc.scalar.copy(result[:], values)
-            nc.scalar.activation(gate[:], gate[:], SIGMOID)
-            weighted = turn.tile([P, span], F32, name="weighted")
-            nc.gpsimd.tensor_tensor(
-                weighted[:].rearrange("p (g j) -> p g j", g=group),
-                result[:].rearrange("p (g j) -> p g j", g=group),
-                wgo_sb[c][:, j0 : j0 + width].rearrange("p (g j) -> p g j", g=1).to_broadcast([P, group, width]),
-                MULT,
-            )
-            gated = result[:] if reuse is None else reuse
+            last = b0 == BLOCKS - 1 and lo + width == J
             if not last:
-                nc.gpsimd.tensor_tensor(gated, weighted[:], gate[:], MULT)
+                nc.gpsimd.tensor_tensor(gated, weighted, gate, MULT)
             for g in range(group):
                 b = b0 + g
                 target = pages[b][:].indirect(places[:, lo // 16 : (lo + width) // 16])
                 if last:
-                    nc.vector.tensor_tensor(target, weighted[:], gate[:], MULT)
+                    nc.vector.tensor_tensor(target, weighted, gate, MULT)
                 else:
                     nc.vector.tensor_copy(target, gated[:, g * width : (g + 1) * width])
                 if lo + width == J:
                     nc.sync.dma_start(out[b * P : (b + 1) * P, :], pages[b][:])
 
-        chunks = range(len(CHUNKS))
         gather(0, 0, EARLY)
         gather(0, EARLY, J)
         gather(1, 0, J // 2)
         gather(1, J // 2, J)
-        for c in chunks:
-            weave(c, 0)
+        for q in range(J // small):
+            weave(q, 0)
         gather(2, 0, J)
-        small = CHUNKS[0][1]
-        for c in (0, 1):
-            gather(PACK - 1, *CHUNKS[c])
-            weave(c, 2)
-            quantize(c)
-        banks = [multiply(c, b0) for c in (0, 1) for b0 in (0, 2)]
-        gather(PACK - 1, *CHUNKS[2])
-        early = [(0, 0, 1, 0, 0), (0, 1, 1, 0, small), (0, 2, 2, 1, 0), (1, 0, 2, 2, 0), (1, 2, 2, 3, 0)]
-        gates = [score(c, b0, group, 0, small, banks[n][0][:, at : at + group * small]) for c, b0, group, n, at in early]
-        after_quantize = grouped[2].rearrange("p j t -> p (j t)").bitcast(F32)[:, :BANK]
-        for count, (c, b0, group, n, at) in enumerate(early):
-            values = banks[n][1][:, at : at + group * small]
-            finish(c, b0, group, 0, small, gates[count], values, False, after_quantize if count == 2 else None)
-            if count == 1:
-                weave(2, 2)
-                quantize(2)
-        for b0 in range(BLOCKS):
-            keys, values = multiply(2, b0)
-            width = BANK if b0 < BLOCKS - 1 else LAST
-            for j0 in range(0, BANK, width):
-                cols = slice(j0, j0 + width)
-                gate = score(2, b0, 1, j0, width, keys[:, cols])
-                finish(2, b0, 1, j0, width, gate, values[:, cols], b0 == BLOCKS - 1 and j0 + width == BANK)
+        last_plane = PACK - 1
+        for c in range(len(CHUNKS)):
+            gather(last_plane, *CHUNKS[c])
+        for q in range(J // small - 1):
+            weave(q, 2)
+            quantize(q)
+        nc.vector.tensor_copy(
+            grouped[-1][:, :, 2:].rearrange("p (c i) t -> p c i t", i=4),
+            picked[1][:, :, J - small :].rearrange("p t (c i) -> p c i t", i=4),
+        )
+        quantize(J // small - 1)
+        early = [(0, 0, 1), (0, 1, 1), (0, 2, 2), (1, 0, 2), (1, 2, 2)]
+        banks = [
+            (multiply(c, b0, "rows", wv_sb, wv_sc, 2, FP4X4), keys_of(c, b0)) for c, b0 in ((0, 0), (0, 2), (1, 0))
+        ]
+
+        def gate_of(c, b0, group):
+            at = (c * BLOCKS + b0) * small
+            return gates[:, at : at + group * small]
+
+        for c, b0, group in early:
+            if 2 * c + b0 // 2 == len(banks):
+                banks.append((None, keys_of(c, b0)))
+            keys = banks[2 * c + b0 // 2][1][:, b0 % 2 * small : (b0 % 2 + group) * small]
+            nc.vector.tensor_tensor(gate_of(c, b0, group), keys, state_of(c, b0, group, 0, small), MULT)
+        weighted_early = grouped[-1][:].rearrange("p j t -> p (j t)").bitcast(F32)
+        for count, (c, b0, group) in enumerate(early):
+            values = banks[2 * c + b0 // 2][0]
+            if values is None:
+                values = multiply(c, b0, "rows", wv_sb, wv_sc, 2, FP4X4)
+            gate = gate_of(c, b0, group)
+            cols = slice(b0 % 2 * small, (b0 % 2 + group) * small)
+            values = out_of_psum(values[:, cols], f"values{count}")
+            nc.scalar.activation(gate, gate, SIGMOID)
+            nc.gpsimd.tensor_tensor(
+                weighted_early[:, cols].rearrange("p (g j) -> p g j", g=group),
+                values[:].rearrange("p (g j) -> p g j", g=group),
+                wgo_first[c][:].rearrange("p (g j) -> p g j", g=1).to_broadcast([P, group, small]),
+                MULT,
+            )
+            finish(c, b0, group, 0, small, gate, weighted_early[:, cols], values[:])
+        scaled = weighted_t(2)
+        for b in range(BLOCKS):
+            keys = keys_of(2, b)
+            values = turn_back(scaled, b, 1)
+            piece = LAST if b == BLOCKS - 1 else BANK
+            for j0 in range(0, BANK, piece):
+                cols = slice(j0, j0 + piece)
+                gate = gate_of(1, b % 2 * 2, 2)[:, cols]
+                keys_sb = out_of_psum(keys[:, cols], f"keys{b}_{j0}")
+                nc.gpsimd.tensor_tensor(gate, keys_sb[:], state_of(2, b, 1, j0, piece), MULT)
+                weighted = out_of_psum(values[:, cols], f"weighted{b}_{j0}")
+                nc.scalar.activation(gate, gate, SIGMOID)
+                finish(2, b, 1, j0, piece, gate, weighted[:], weighted[:])

@@ -12,7 +12,7 @@ GROUP = P // GROUPS
 BANK = 512
 CHUNKS = ((0, 256), (256, 512), (512, 1024))
 WEAVE = 128
-EARLY = 384
+EARLY = 256
 LAST = 256
 FLOPS = 2 * 2 * K * N * J
 
@@ -35,14 +35,15 @@ def tile_list_sigS_kernel(
     nc = tc.nc
     with ExitStack() as ctx:
         held = ctx.enter_context(tc.tile_pool(name="held", bufs=1))
-        psum = ctx.enter_context(tc.psum_pool(name="psum", bufs=3))
-        psum_t = ctx.enter_context(tc.psum_pool(name="psum_t", bufs=2))
+        psum = ctx.enter_context(tc.psum_pool(name="psum", bufs=4))
+        psum_k = ctx.enter_context(tc.psum_pool(name="psum_k", bufs=4))
 
         small = CHUNKS[0][1]
         picks = held.tile([P, J // 16], U16, name="picks")
         places = held.tile([P, J // 16], U16, name="places")
         wgt_sb = held.tile([P, J], F32, name="wgt_sb")
-        wgo_first = [held.tile([P, small], F32, name=f"wgo_first{c}") for c in (0, 1)]
+        wgo_first = held.tile([P, 2 * small], F32, name="wgo_first")
+        wgt_rows = held.tile([P, P], F32, name="wgt_rows")
         wgo_rows = held.tile([P, P], F32, name="wgo_rows")
         wgo_t = held.tile([P, P], F32, name="wgo_t")
         identity = held.tile([P, P], F32, name="identity")
@@ -54,7 +55,7 @@ def tile_list_sigS_kernel(
         wk_sc = held.tile([P, N], U8, name="wk_sc", align_bytes=64)
         wv_sc = held.tile([P, N], U8, name="wv_sc", align_bytes=64)
 
-        for plane_sc, scales, queue in ((wv_sc, wv_scales, nc.scalar), (wk_sc, wk_scales, nc.gpsimd)):
+        def load_scales(queue, plane_sc, scales):
             for q in range(4):
                 queue.dma_start(
                     plane_sc[32 * q : 32 * q + 4, :].bitcast(I32),
@@ -62,50 +63,68 @@ def tile_list_sigS_kernel(
                 )
 
         warm = held.tile([P, 1], F32, name="warm")
-        nc.vector.memset(warm[:], 0.0)
+        nc.gpsimd.memset(warm[:], 0.0)
         nc.scalar.activation(warm[:], warm[:], SIGMOID)
+
+        make_identity(nc, identity[:])
+        load_scales(nc.gpsimd, wk_sc, wk_scales)
+        load_scales(nc.scalar, wv_sc, wv_scales)
 
         x_planes = xT.rearrange("(p i) t -> i p t", i=PACK)
         st_blocks = st.rearrange("(b p) j -> p b j", p=P)
+        nc.sync.dma_start(wgt_rows[:], wgt.rearrange("(h r) (u j) -> r h u j", r=8, j=P)[0])
         nc.sync.dma_start(picks[:], offs)
-        nc.sync.dma_start(wgt_sb[:, :EARLY], wgt[:, :EARLY])
-        nc.sync.dma_start(planes[0][:], x_planes[0])
-        nc.sync.dma_start(wgt_sb[:, EARLY:], wgt[:, EARLY:])
-        nc.sync.dma_start(planes[1][:], x_planes[1])
-        nc.sync.dma_start(wgo_rows[:], wgo.rearrange("(h r) (u j) -> r h u j", r=8, j=P)[0])
-        for i in range(2, PACK):
+        for i in range(PACK):
             nc.sync.dma_start(planes[i][:], x_planes[i])
+            if i == 1:
+                nc.sync.dma_start(wgo_rows[:], wgo.rearrange("(h r) (u j) -> r h u j", r=8, j=P)[0])
         nc.sync.dma_start(wv_sb[:].bitcast(I32), wv_words[0].bitcast(I32))
         nc.sync.dma_start(wk_sb[:].bitcast(I32), wk_words[0].rearrange("p n t -> p (n t)").bitcast(I32))
         nc.sync.dma_start(states[0][:], st_blocks[:, :, :small])
-        nc.sync.dma_start(wgo_first[0][:], wgo[:, :small])
-        nc.sync.dma_start(places[:], offs2)
+        nc.sync.dma_start(wgo_first[:], wgo[:, : 2 * small])
         nc.sync.dma_start(states[1][:], st_blocks[:, :, small : 2 * small])
-        nc.sync.dma_start(wgo_first[1][:], wgo[:, small : 2 * small])
+        nc.sync.dma_start(places[:], offs2)
         nc.sync.dma_start(states[2][:], st_blocks[:, :, 2 * small :])
 
-        make_identity(nc, identity[:])
-        for b in range(BLOCKS):
-            (nc.vector if b < 2 else nc.gpsimd).memset(pages[b][:], 0.0)
         turned = psum.tile([P, BANK], F32, name="rows")
-        nc.tensor.transpose(turned[:, :P], wgo_rows[:], identity[:])
-        nc.scalar.copy(wgo_t[:], turned[:, :P])
+        nc.tensor.transpose(turned[:, :P], wgt_rows[:], identity[:])
 
-        picked = [held.tile([P, 2, J], F32, name=f"picked{h}", align_bytes=64) for h in range(PACK // 2)]
-        grouped = [held.tile([P, small, PACK], BF16, name=f"grouped{q}", align_bytes=64) for q in range(J // small)]
+        def spread(columns, u0, tiles, target, copy):
+            wide = held.tile([P, tiles, 16, 8], F32, name=f"wide_{target.shape[1]}_{u0}")
+            by_tile = columns.rearrange("p (h u) -> p u h", h=16)[:, u0 : u0 + tiles, :]
+            copy(wide[:], by_tile.unsqueeze(3).to_broadcast([P, tiles, 16, 8]))
+            bank = psum_k.tile([P, BANK], F32, name="keys")
+            for u in range(tiles):
+                nc.tensor.transpose(
+                    bank[:, u * P : (u + 1) * P], wide[:, u].rearrange("p g r -> p (g r)"), identity[:]
+                )
+            nc.scalar.copy(target[:, u0 * P : (u0 + tiles) * P], bank[:, : tiles * P])
+            return bank
+
+        for u0, tiles in ((0, 2), (2, 2), (4, 4)):
+            bank = spread(turned[:, :P], u0, tiles, wgt_sb, nc.vector.tensor_copy)
+        nc.tensor.transpose(bank[:, :P], wgo_rows[:], identity[:])
+        nc.scalar.copy(wgo_t[:], bank[:, :P])
+
+        for b in range(BLOCKS):
+            nc.gpsimd.memset(pages[b][:], 0.0)
+        picked = held.tile([P, PACK, J], F32, name="picked")
+        grouped = [held.tile([P, small, PACK], BF16, name=f"grouped{q}", align_bytes=64)[:] for q in range(J // small - 1)]
+        grouped.append(grouped[0])
         codes = [held.tile([P, hi - lo], U32, name=f"codes{lo}", align_bytes=64) for lo, hi in CHUNKS]
         code_sc = [held.tile([P, hi - lo], U8, name=f"code_sc{lo}", align_bytes=64) for lo, hi in CHUNKS]
+        scores = held.tile([P, 3 * BANK], F32, name="scores")
         gates = held.tile([P, 4 * BANK], F32, name="gates")
 
         def gather(i, lo, hi):
             window = planes[i][:].indirect(picks[:, lo // 16 : hi // 16])
-            nc.vector.tensor_tensor(picked[i // 2][:, i % 2, lo:hi], window, wgt_sb[:, lo:hi], MULT)
+            nc.vector.tensor_tensor(picked[:, i, lo:hi], window, wgt_sb[:, lo:hi], MULT)
 
         def weave(q, i0):
             for j0 in range(0, small, WEAVE):
                 nc.scalar.copy(
                     grouped[q][:, j0 : j0 + WEAVE, i0 : i0 + 2].rearrange("p (c i) t -> p c i t", i=4),
-                    picked[i0 // 2][:, :, q * small + j0 : q * small + j0 + WEAVE].rearrange("p t (c i) -> p c i t", i=4),
+                    picked[:, i0 : i0 + 2, q * small + j0 : q * small + j0 + WEAVE].rearrange("p t (c i) -> p c i t", i=4),
                 )
 
         def quantize(q):
@@ -114,12 +133,12 @@ def tile_list_sigS_kernel(
             nc.vector.quantize_mx(
                 out=codes[c][:, cols].bitcast(FP8X4),
                 scales=code_sc[c][:, cols],
-                in_=grouped[q][:].rearrange("p j t -> p (j t)"),
+                in_=grouped[q].rearrange("p j t -> p (j t)"),
             )
 
-        def multiply(c, b0, name, words, scales, size, view):
+        def multiply(c, b0, pool, name, words, scales, size, view):
             width = CHUNKS[c][1] - CHUNKS[c][0]
-            bank = psum.tile([P, BANK], F32, name=name)
+            bank = pool.tile([P, BANK], F32, name=name)
             for g in range(BANK // width):
                 rows = slice((b0 + g) * P, (b0 + g + 1) * P)
                 nc.tensor.matmul_mx(
@@ -134,14 +153,14 @@ def tile_list_sigS_kernel(
             return bank
 
         def keys_of(c, b0):
-            return multiply(c, b0, "keys", wk_sb, wk_sc, 1, FP8X4)
+            return multiply(c, b0, psum_k, "keys", wk_sb, wk_sc, 1, FP8X4)
 
         def weighted_t(c):
             lo, hi = CHUNKS[c]
-            scaled = held.tile([P, (hi - lo) // P, N], F32, name=f"scaled{lo}")
+            scaled = [held.tile([P, N], F32, name=f"scaled{u}")[:] for u in range((hi - lo) // P)]
             for u in range((hi - lo) // P):
                 entries = slice(u * P, (u + 1) * P)
-                bank = psum_t.tile([P, N], F32, name="values_t")
+                bank = psum_k.tile([P, N], F32, name="keys")
                 nc.tensor.matmul_mx(
                     out=bank[:],
                     lhsT=codes[c][:, entries].bitcast(FP8X4),
@@ -155,7 +174,7 @@ def tile_list_sigS_kernel(
                     rows = slice(g * GROUP, (g + 1) * GROUP)
                     column = 2 * g * (J // P) + lo // P + u
                     nc.scalar.activation(
-                        scaled[:, u, :].rearrange("p (b r) -> p b r", r=P)[:, :, rows],
+                        scaled[u].rearrange("p (b r) -> p b r", r=P)[:, :, rows],
                         bank[:].rearrange("p (b r) -> p b r", r=P)[:, :, rows],
                         COPY,
                         scale=wgo_t[:, column : column + 1],
@@ -163,13 +182,13 @@ def tile_list_sigS_kernel(
             return scaled
 
         def turn_back(scaled, b0, group):
-            tiles = scaled.shape[1]
+            tiles = len(scaled)
             bank = psum.tile([P, BANK], F32, name="rows")
             for g in range(group):
                 for u in range(tiles):
                     at = (g * tiles + u) * P
                     nc.tensor.transpose(
-                        bank[:, at : at + P], scaled[:, u, (b0 + g) * P : (b0 + g + 1) * P], identity[:]
+                        bank[:, at : at + P], scaled[u][:, (b0 + g) * P : (b0 + g + 1) * P], identity[:]
                     )
             return bank
 
@@ -179,7 +198,7 @@ def tile_list_sigS_kernel(
             return landed
 
         def state_of(c, b0, group, j0, width):
-            return states[c][:, b0 : b0 + group, j0 : j0 + width].rearrange("p g j -> p (g j)")
+            return states[c][:, b0 : b0 + group, j0 : j0 + width]
 
         def finish(c, b0, group, j0, width, gate, weighted, gated):
             lo = CHUNKS[c][0] + j0
@@ -197,10 +216,11 @@ def tile_list_sigS_kernel(
                     nc.sync.dma_start(out[b * P : (b + 1) * P, :], pages[b][:])
 
         gather(0, 0, EARLY)
-        gather(0, EARLY, J)
+        gather(0, EARLY, J // 2)
+        gather(0, J // 2, J)
         gather(1, 0, J // 2)
         gather(1, J // 2, J)
-        for q in range(J // small):
+        for q in range(J // small - 1):
             weave(q, 0)
         gather(2, 0, J)
         last_plane = PACK - 1
@@ -210,40 +230,50 @@ def tile_list_sigS_kernel(
             weave(q, 2)
             quantize(q)
         nc.vector.tensor_copy(
-            grouped[-1][:, :, 2:].rearrange("p (c i) t -> p c i t", i=4),
-            picked[1][:, :, J - small :].rearrange("p t (c i) -> p c i t", i=4),
+            grouped[-1].rearrange("p (c i) t -> p c t i", i=4),
+            picked[:, :, J - small :].rearrange("p t (c i) -> p c t i", i=4),
         )
         quantize(J // small - 1)
         early = [(0, 0, 1), (0, 1, 1), (0, 2, 2), (1, 0, 2), (1, 2, 2)]
-        banks = [
-            (multiply(c, b0, "rows", wv_sb, wv_sc, 2, FP4X4), keys_of(c, b0)) for c, b0 in ((0, 0), (0, 2), (1, 0))
-        ]
+        value_banks = [multiply(0, 0, psum, "rows", wv_sb, wv_sc, 2, FP4X4)]
+        key_banks = [keys_of(c, b0) for c in (0, 1) for b0 in (0, 2)]
 
         def gate_of(c, b0, group):
             at = (c * BLOCKS + b0) * small
             return gates[:, at : at + group * small]
 
+        def score_of(c, b0, group):
+            at = (c * BLOCKS + b0) * small
+            return scores[:, at : at + group * small] if at < 3 * BANK else gate_of(c, b0, group)
+
         for c, b0, group in early:
-            if 2 * c + b0 // 2 == len(banks):
-                banks.append((None, keys_of(c, b0)))
-            keys = banks[2 * c + b0 // 2][1][:, b0 % 2 * small : (b0 % 2 + group) * small]
-            nc.vector.tensor_tensor(gate_of(c, b0, group), keys, state_of(c, b0, group, 0, small), MULT)
-        weighted_early = grouped[-1][:].rearrange("p j t -> p (j t)").bitcast(F32)
-        for count, (c, b0, group) in enumerate(early):
-            values = banks[2 * c + b0 // 2][0]
-            if values is None:
-                values = multiply(c, b0, "rows", wv_sb, wv_sc, 2, FP4X4)
-            gate = gate_of(c, b0, group)
-            cols = slice(b0 % 2 * small, (b0 % 2 + group) * small)
-            values = out_of_psum(values[:, cols], f"values{count}")
-            nc.scalar.activation(gate, gate, SIGMOID)
-            nc.gpsimd.tensor_tensor(
-                weighted_early[:, cols].rearrange("p (g j) -> p g j", g=group),
-                values[:].rearrange("p (g j) -> p g j", g=group),
-                wgo_first[c][:].rearrange("p (g j) -> p g j", g=1).to_broadcast([P, group, small]),
+            keys = key_banks[2 * c + b0 // 2][:, b0 % 2 * small : (b0 % 2 + group) * small]
+            nc.vector.tensor_tensor(
+                score_of(c, b0, group).rearrange("p (g j) -> p g j", g=group),
+                keys.rearrange("p (g j) -> p g j", g=group),
+                state_of(c, b0, group, 0, small),
                 MULT,
             )
-            finish(c, b0, group, 0, small, gate, weighted_early[:, cols], values[:])
+        weighted_early = grouped[-1].rearrange("p j t -> p (j t)").bitcast(F32)
+        for count, (c, b0, group) in enumerate(early):
+            if 2 * c + b0 // 2 == len(value_banks):
+                value_banks.append(multiply(c, b0, psum, "rows", wv_sb, wv_sc, 2, FP4X4))
+            values = value_banks[2 * c + b0 // 2]
+            gate = gate_of(c, b0, group)
+            cols = slice(b0 % 2 * small, (b0 % 2 + group) * small)
+            if count >= 2:
+                bank, values = values, scores[:, (count - 2) * BANK : (count - 1) * BANK]
+                nc.scalar.copy(values, bank[:])
+            else:
+                values = out_of_psum(values[:, cols], f"values{count}")[:]
+            nc.scalar.activation(gate, score_of(c, b0, group), SIGMOID)
+            nc.gpsimd.tensor_tensor(
+                weighted_early[:, cols].rearrange("p (g j) -> p g j", g=group),
+                values.rearrange("p (g j) -> p g j", g=group),
+                wgo_first[:, c * small : (c + 1) * small].rearrange("p (g j) -> p g j", g=1).to_broadcast([P, group, small]),
+                MULT,
+            )
+            finish(c, b0, group, 0, small, gate, weighted_early[:, cols], values)
         scaled = weighted_t(2)
         for b in range(BLOCKS):
             keys = keys_of(2, b)
@@ -253,7 +283,7 @@ def tile_list_sigS_kernel(
                 cols = slice(j0, j0 + piece)
                 gate = gate_of(1, b % 2 * 2, 2)[:, cols]
                 keys_sb = out_of_psum(keys[:, cols], f"keys{b}_{j0}")
-                nc.gpsimd.tensor_tensor(gate, keys_sb[:], state_of(2, b, 1, j0, piece), MULT)
+                nc.gpsimd.tensor_tensor(gate, keys_sb[:], state_of(2, b, 1, j0, piece)[:, 0], MULT)
                 weighted = out_of_psum(values[:, cols], f"weighted{b}_{j0}")
                 nc.scalar.activation(gate, gate, SIGMOID)
                 finish(2, b, 1, j0, piece, gate, weighted[:], weighted[:])

@@ -13,7 +13,7 @@ BANK = 512
 CHUNKS = ((0, 256), (256, 512), (512, 1024))
 WEAVE = 128
 EARLY = 256
-LAST = 256
+LAST = 512
 FLOPS = 2 * 2 * K * N * J
 
 F32 = mybir.dt.float32
@@ -36,7 +36,7 @@ def tile_list_sigS_kernel(
     with ExitStack() as ctx:
         held = ctx.enter_context(tc.tile_pool(name="held", bufs=1))
         psum = ctx.enter_context(tc.psum_pool(name="psum", bufs=4))
-        psum_k = ctx.enter_context(tc.psum_pool(name="psum_k", bufs=4))
+        psum_k = ctx.enter_context(tc.psum_pool(name="psum_k", bufs=3))
 
         small = CHUNKS[0][1]
         picks = held.tile([P, J // 16], U16, name="picks")
@@ -108,13 +108,15 @@ def tile_list_sigS_kernel(
 
         for b in range(BLOCKS):
             nc.gpsimd.memset(pages[b][:], 0.0)
-        picked = held.tile([P, PACK, J], F32, name="picked")
-        grouped = [held.tile([P, small, PACK], BF16, name=f"grouped{q}", align_bytes=64)[:] for q in range(J // small - 1)]
-        grouped.append(grouped[0])
+        picked_and_more = held.tile([P, PACK * J + small], F32, name="picked", align_bytes=64)
+        picked = picked_and_more[:, : PACK * J].rearrange("p (t j) -> p t j", t=PACK)
+        grouped = [picked_and_more[:, PACK * J - small :].bitcast(BF16).rearrange("p (j t) -> p j t", t=PACK)] + [
+            held.tile([P, small, PACK], BF16, name=f"grouped{q}", align_bytes=64)[:] for q in range(1, J // small)
+        ]
         codes = [held.tile([P, hi - lo], U32, name=f"codes{lo}", align_bytes=64) for lo, hi in CHUNKS]
         code_sc = [held.tile([P, hi - lo], U8, name=f"code_sc{lo}", align_bytes=64) for lo, hi in CHUNKS]
-        scores = held.tile([P, 3 * BANK], F32, name="scores")
-        gates = held.tile([P, 4 * BANK], F32, name="gates")
+        scores = held.tile([P, 2 * BANK], F32, name="scores")
+        gates = held.tile([P, 3 * BANK], F32, name="gates")
 
         def gather(i, lo, hi):
             window = planes[i][:].indirect(picks[:, lo // 16 : hi // 16])
@@ -220,23 +222,20 @@ def tile_list_sigS_kernel(
         gather(0, J // 2, J)
         gather(1, 0, J // 2)
         gather(1, J // 2, J)
-        for q in range(J // small - 1):
+        for q in range(J // small):
             weave(q, 0)
         gather(2, 0, J)
         last_plane = PACK - 1
-        for c in range(len(CHUNKS)):
-            gather(last_plane, *CHUNKS[c])
-        for q in range(J // small - 1):
-            weave(q, 2)
-            quantize(q)
-        nc.vector.tensor_copy(
-            grouped[-1].rearrange("p (c i) t -> p c t i", i=4),
-            picked[:, :, J - small :].rearrange("p t (c i) -> p c t i", i=4),
-        )
-        quantize(J // small - 1)
-        early = [(0, 0, 1), (0, 1, 1), (0, 2, 2), (1, 0, 2), (1, 2, 2)]
+        gather(last_plane, 0, small)
+        gather(last_plane, small, J - small)
+        weave(0, 2)
+        quantize(0)
+        gather(last_plane, J - small, J)
+        weave(1, 2)
+        quantize(1)
+        early = [(0, 0, 1), (0, 1, 1), (0, 2, 2), (1, 0, 2)]
         value_banks = [multiply(0, 0, psum, "rows", wv_sb, wv_sc, 2, FP4X4)]
-        key_banks = [keys_of(c, b0) for c in (0, 1) for b0 in (0, 2)]
+        key_banks = [keys_of(c, b0) for c, b0 in ((0, 0), (0, 2), (1, 0))]
 
         def gate_of(c, b0, group):
             at = (c * BLOCKS + b0) * small
@@ -244,7 +243,7 @@ def tile_list_sigS_kernel(
 
         def score_of(c, b0, group):
             at = (c * BLOCKS + b0) * small
-            return scores[:, at : at + group * small] if at < 3 * BANK else gate_of(c, b0, group)
+            return scores[:, at : at + group * small] if at < 2 * BANK else gate_of(c, b0, group)
 
         for c, b0, group in early:
             keys = key_banks[2 * c + b0 // 2][:, b0 % 2 * small : (b0 % 2 + group) * small]
@@ -254,36 +253,67 @@ def tile_list_sigS_kernel(
                 state_of(c, b0, group, 0, small),
                 MULT,
             )
-        weighted_early = grouped[-1].rearrange("p j t -> p (j t)").bitcast(F32)
+        weighted_early = held.tile([P, BANK], F32, name="weighted_early")
+        after_quantize = grouped[-1].rearrange("p j t -> p (j t)").bitcast(F32)
+
+        def weigh(c, group, weighted, values, engine=nc.gpsimd):
+            engine.tensor_tensor(
+                weighted.rearrange("p (g j) -> p g j", g=group),
+                values.rearrange("p (g j) -> p g j", g=group),
+                wgo_first[:, c * small : (c + 1) * small].unsqueeze(1).to_broadcast([P, group, small]),
+                MULT,
+            )
+
         for count, (c, b0, group) in enumerate(early):
             if 2 * c + b0 // 2 == len(value_banks):
                 value_banks.append(multiply(c, b0, psum, "rows", wv_sb, wv_sc, 2, FP4X4))
             values = value_banks[2 * c + b0 // 2]
             gate = gate_of(c, b0, group)
             cols = slice(b0 % 2 * small, (b0 % 2 + group) * small)
-            if count >= 2:
-                bank, values = values, scores[:, (count - 2) * BANK : (count - 1) * BANK]
+            weighted = weighted_early[:, cols]
+            if count == 2:
+                weighted = scores[:, :BANK]
+                weigh(c, group, weighted, values[:], nc.vector)
+            elif count == 3:
+                bank, values = values, scores[:, BANK:]
                 nc.scalar.copy(values, bank[:])
             else:
                 values = out_of_psum(values[:, cols], f"values{count}")[:]
             nc.scalar.activation(gate, score_of(c, b0, group), SIGMOID)
-            nc.gpsimd.tensor_tensor(
-                weighted_early[:, cols].rearrange("p (g j) -> p g j", g=group),
-                values.rearrange("p (g j) -> p g j", g=group),
-                wgo_first[:, c * small : (c + 1) * small].rearrange("p (g j) -> p g j", g=1).to_broadcast([P, group, small]),
-                MULT,
-            )
-            finish(c, b0, group, 0, small, gate, weighted_early[:, cols], values)
+            if count != 2:
+                weigh(c, group, weighted, values)
+            finish(c, b0, group, 0, small, gate, weighted, after_quantize if count == 2 else values)
+            if count < 2:
+                weave(2 + count, 2)
+                quantize(2 + count)
         scaled = weighted_t(2)
+        turns = [gates[:, 2 * BANK :], weighted_early[:]]
+        freed = []
         for b in range(BLOCKS):
+            if b == 2:
+                keys_sb = out_of_psum(keys_of(1, 2)[:], "keys_late")
+                gate = turns[0]
+                turns.reverse()
+                nc.gpsimd.tensor_tensor(
+                    gate.rearrange("p (g j) -> p g j", g=2),
+                    keys_sb[:].rearrange("p (g j) -> p g j", g=2),
+                    state_of(1, 2, 2, 0, small),
+                    MULT,
+                )
+                values = out_of_psum(multiply(1, 2, psum, "rows", wv_sb, wv_sc, 2, FP4X4)[:], "values_late")
+                nc.scalar.activation(gate, gate, SIGMOID)
+                weigh(1, 2, freed[0][:], values[:])
+                finish(1, 2, 2, 0, small, gate, freed[0][:], values[:])
             keys = keys_of(2, b)
             values = turn_back(scaled, b, 1)
             piece = LAST if b == BLOCKS - 1 else BANK
             for j0 in range(0, BANK, piece):
                 cols = slice(j0, j0 + piece)
-                gate = gate_of(1, b % 2 * 2, 2)[:, cols]
+                gate = turns[0][:, cols]
                 keys_sb = out_of_psum(keys[:, cols], f"keys{b}_{j0}")
                 nc.gpsimd.tensor_tensor(gate, keys_sb[:], state_of(2, b, 1, j0, piece)[:, 0], MULT)
                 weighted = out_of_psum(values[:, cols], f"weighted{b}_{j0}")
                 nc.scalar.activation(gate, gate, SIGMOID)
-                finish(2, b, 1, j0, piece, gate, weighted[:], weighted[:])
+                finish(2, b, 1, j0, piece, gate, weighted[:], keys_sb[:])
+                freed.append(weighted)
+            turns.reverse()

@@ -11,9 +11,8 @@ GROUPS = 8
 GROUP = P // GROUPS
 BANK = 512
 CHUNKS = ((0, 256), (256, 512), (512, 1024))
-WEAVE = 128
-EARLY = 256
-LAST = 512
+WEAVE = 256
+EARLY = 128
 FLOPS = 2 * 2 * K * N * J
 
 F32 = mybir.dt.float32
@@ -35,8 +34,9 @@ def tile_list_sigS_kernel(
     nc = tc.nc
     with ExitStack() as ctx:
         held = ctx.enter_context(tc.tile_pool(name="held", bufs=1))
-        psum = ctx.enter_context(tc.psum_pool(name="psum", bufs=4))
+        psum = ctx.enter_context(tc.psum_pool(name="psum", bufs=3))
         psum_k = ctx.enter_context(tc.psum_pool(name="psum_k", bufs=3))
+        psum_first = ctx.enter_context(tc.psum_pool(name="psum_first", bufs=1))
 
         small = CHUNKS[0][1]
         picks = held.tile([P, J // 16], U16, name="picks")
@@ -49,7 +49,10 @@ def tile_list_sigS_kernel(
         identity = held.tile([P, P], F32, name="identity")
         planes = [held.tile([P, T], F32, name=f"plane{i}") for i in range(PACK)]
         pages = [held.tile([P, T], F32, name=f"page{b}") for b in range(BLOCKS)]
-        states = [held.tile([P, BLOCKS, hi - lo], F32, name=f"state{lo}") for lo, hi in CHUNKS]
+        state_first = held.tile([P, 2, BANK], F32, name="state_first")
+        state_third = held.tile([P, BANK], F32, name="state_third")
+        state_late = held.tile([P, BLOCKS - 1, BANK], F32, name="state_late")
+        state_last = held.tile([P, J], F32, name="state_last")
         wk_sb = held.tile([P, N], U32, name="wk_sb", align_bytes=64)
         wv_sb = held.tile([P, 2 * N], U8, name="wv_sb", align_bytes=64)
         wk_sc = held.tile([P, N], U8, name="wk_sc", align_bytes=64)
@@ -80,11 +83,12 @@ def tile_list_sigS_kernel(
                 nc.sync.dma_start(wgo_rows[:], wgo.rearrange("(h r) (u j) -> r h u j", r=8, j=P)[0])
         nc.sync.dma_start(wv_sb[:].bitcast(I32), wv_words[0].bitcast(I32))
         nc.sync.dma_start(wk_sb[:].bitcast(I32), wk_words[0].rearrange("p n t -> p (n t)").bitcast(I32))
-        nc.sync.dma_start(states[0][:], st_blocks[:, :, :small])
+        nc.sync.dma_start(state_first[:], st_blocks[:, :2, :BANK])
         nc.sync.dma_start(wgo_first[:], wgo[:, : 2 * small])
-        nc.sync.dma_start(states[1][:], st_blocks[:, :, small : 2 * small])
+        nc.sync.dma_start(state_third[:], st_blocks[:, 2, :BANK])
         nc.sync.dma_start(places[:], offs2)
-        nc.sync.dma_start(states[2][:], st_blocks[:, :, 2 * small :])
+        nc.sync.dma_start(state_late[:], st_blocks[:, : BLOCKS - 1, BANK:])
+        nc.sync.dma_start(state_last[:], st_blocks[:, BLOCKS - 1, :])
 
         turned = psum.tile([P, BANK], F32, name="rows")
         nc.tensor.transpose(turned[:, :P], wgt_rows[:], identity[:])
@@ -101,7 +105,7 @@ def tile_list_sigS_kernel(
             nc.scalar.copy(target[:, u0 * P : (u0 + tiles) * P], bank[:, : tiles * P])
             return bank
 
-        for u0, tiles in ((0, 2), (2, 2), (4, 4)):
+        for u0, tiles in ((0, 1), (1, 3), (4, 4)):
             bank = spread(turned[:, :P], u0, tiles, wgt_sb, nc.vector.tensor_copy)
         nc.tensor.transpose(bank[:, :P], wgo_rows[:], identity[:])
         nc.scalar.copy(wgo_t[:], bank[:, :P])
@@ -138,24 +142,30 @@ def tile_list_sigS_kernel(
                 in_=grouped[q].rearrange("p j t -> p (j t)"),
             )
 
-        def multiply(c, b0, pool, name, words, scales, size, view):
-            width = CHUNKS[c][1] - CHUNKS[c][0]
-            bank = pool.tile([P, BANK], F32, name=name)
-            for g in range(BANK // width):
-                rows = slice((b0 + g) * P, (b0 + g + 1) * P)
-                nc.tensor.matmul_mx(
-                    out=bank[:, g * width : (g + 1) * width],
-                    lhsT=words[:, size * rows.start : size * rows.stop].bitcast(view),
-                    lhsT_scale=scales[:, rows],
-                    rhs=codes[c][:].bitcast(FP8X4),
-                    rhs_scale=code_sc[c][:],
-                    start=True,
-                    stop=True,
-                )
+        def multiply(bank, at, b, c, words, scales, size, view):
+            lo, hi = CHUNKS[c]
+            rows = slice(b * P, (b + 1) * P)
+            nc.tensor.matmul_mx(
+                out=bank[:, at : at + hi - lo],
+                lhsT=words[:, size * rows.start : size * rows.stop].bitcast(view),
+                lhsT_scale=scales[:, rows],
+                rhs=codes[c][:].bitcast(FP8X4),
+                rhs_scale=code_sc[c][:],
+                start=True,
+                stop=True,
+            )
+
+        def keys_of(parts):
+            bank = psum_k.tile([P, BANK], F32, name="keys")
+            for n, (b, c) in enumerate(parts):
+                multiply(bank, n * small, b, c, wk_sb, wk_sc, 1, FP8X4)
             return bank
 
-        def keys_of(c, b0):
-            return multiply(c, b0, psum_k, "keys", wk_sb, wk_sc, 1, FP8X4)
+        def values_of(parts):
+            bank = psum.tile([P, BANK], F32, name="rows")
+            for n, (b, c) in enumerate(parts):
+                multiply(bank, n * small, b, c, wv_sb, wv_sc, 2, FP4X4)
+            return bank
 
         def weighted_t(c):
             lo, hi = CHUNKS[c]
@@ -199,23 +209,10 @@ def tile_list_sigS_kernel(
             nc.scalar.copy(landed[:], bank)
             return landed
 
-        def state_of(c, b0, group, j0, width):
-            return states[c][:, b0 : b0 + group, j0 : j0 + width]
-
-        def finish(c, b0, group, j0, width, gate, weighted, gated):
-            lo = CHUNKS[c][0] + j0
-            last = b0 == BLOCKS - 1 and lo + width == J
-            if not last:
-                nc.gpsimd.tensor_tensor(gated, weighted, gate, MULT)
-            for g in range(group):
-                b = b0 + g
-                target = pages[b][:].indirect(places[:, lo // 16 : (lo + width) // 16])
-                if last:
-                    nc.vector.tensor_tensor(target, weighted, gate, MULT)
-                else:
-                    nc.vector.tensor_copy(target, gated[:, g * width : (g + 1) * width])
-                if lo + width == J:
-                    nc.sync.dma_start(out[b * P : (b + 1) * P, :], pages[b][:])
+        def scatter(b, lo, hi, gated):
+            nc.vector.tensor_copy(pages[b][:].indirect(places[:, lo // 16 : hi // 16]), gated)
+            if hi == J:
+                nc.sync.dma_start(out[b * P : (b + 1) * P, :], pages[b][:])
 
         gather(0, 0, EARLY)
         gather(0, EARLY, J // 2)
@@ -233,87 +230,77 @@ def tile_list_sigS_kernel(
         gather(last_plane, J - small, J)
         weave(1, 2)
         quantize(1)
-        early = [(0, 0, 1), (0, 1, 1), (0, 2, 2), (1, 0, 2)]
-        value_banks = [multiply(0, 0, psum, "rows", wv_sb, wv_sc, 2, FP4X4)]
-        key_banks = [keys_of(c, b0) for c, b0 in ((0, 0), (0, 2), (1, 0))]
-
-        def gate_of(c, b0, group):
-            at = (c * BLOCKS + b0) * small
-            return gates[:, at : at + group * small]
-
-        def score_of(c, b0, group):
-            at = (c * BLOCKS + b0) * small
-            return scores[:, at : at + group * small] if at < 2 * BANK else gate_of(c, b0, group)
-
-        for c, b0, group in early:
-            keys = key_banks[2 * c + b0 // 2][:, b0 % 2 * small : (b0 % 2 + group) * small]
-            nc.vector.tensor_tensor(
-                score_of(c, b0, group).rearrange("p (g j) -> p g j", g=group),
-                keys.rearrange("p (g j) -> p g j", g=group),
-                state_of(c, b0, group, 0, small),
-                MULT,
-            )
-        weighted_early = held.tile([P, BANK], F32, name="weighted_early")
+        first, second, half = slice(0, small), slice(small, BANK), slice(0, BANK)
+        products = held.tile([P, J], F32, name="products")
+        late = held.tile([P, J], F32, name="late")
         after_quantize = grouped[-1].rearrange("p j t -> p (j t)").bitcast(F32)
 
-        def weigh(c, group, weighted, values, engine=nc.gpsimd):
-            engine.tensor_tensor(
-                weighted.rearrange("p (g j) -> p g j", g=group),
-                values.rearrange("p (g j) -> p g j", g=group),
-                wgo_first[:, c * small : (c + 1) * small].unsqueeze(1).to_broadcast([P, group, small]),
-                MULT,
-            )
+        parts = (((0, 0), (1, 0)), ((0, 1), (1, 1)), ((2, 0), (2, 1)))
+        values_first = psum_first.tile([P, BANK], F32, name="values_first")
+        keys_first = psum_first.tile([P, BANK], F32, name="keys_first")
+        multiply(values_first, 0, 0, 0, wv_sb, wv_sc, 2, FP4X4)
+        multiply(keys_first, 0, 0, 0, wk_sb, wk_sc, 1, FP8X4)
+        values0 = (values_first, values_of(parts[0][1:]))
+        keys = [keys_of(part) for part in (parts[0][1:], parts[1], parts[2])]
+        gate0, gate1, gate3 = gates[:, half], gates[:, BANK:J], gates[:, J:]
+        pair = "p (g j) -> p g j"
+        for b, cols in enumerate((first, second)):
+            bank = (keys_first, keys[0])[b]
+            nc.vector.tensor_tensor(scores[:, cols], bank[:, first], state_first[:, b, first], MULT)
+        nc.vector.tensor_tensor(
+            scores[:, BANK:].rearrange(pair, g=2), keys[1][:].rearrange(pair, g=2), state_first[:, :, second], MULT
+        )
+        nc.vector.tensor_tensor(gate3, keys[2][:], state_third[:], MULT)
 
-        for count, (c, b0, group) in enumerate(early):
-            if 2 * c + b0 // 2 == len(value_banks):
-                value_banks.append(multiply(c, b0, psum, "rows", wv_sb, wv_sc, 2, FP4X4))
-            values = value_banks[2 * c + b0 // 2]
-            gate = gate_of(c, b0, group)
-            cols = slice(b0 % 2 * small, (b0 % 2 + group) * small)
-            weighted = weighted_early[:, cols]
-            if count == 2:
-                weighted = scores[:, :BANK]
-                weigh(c, group, weighted, values[:], nc.vector)
-            elif count == 3:
-                bank, values = values, scores[:, BANK:]
-                nc.scalar.copy(values, bank[:])
-            else:
-                values = out_of_psum(values[:, cols], f"values{count}")[:]
-            nc.scalar.activation(gate, score_of(c, b0, group), SIGMOID)
-            if count != 2:
-                weigh(c, group, weighted, values)
-            finish(c, b0, group, 0, small, gate, weighted, after_quantize if count == 2 else values)
-            if count < 2:
-                weave(2 + count, 2)
-                quantize(2 + count)
+        for b, cols in enumerate((first, second)):
+            landed = out_of_psum(values0[b][:, first], f"values{b}")
+            nc.scalar.activation(gate0[:, cols], scores[:, cols], SIGMOID)
+            nc.gpsimd.tensor_tensor(products[:, cols], landed[:], wgo_first[:, first], MULT)
+            nc.gpsimd.tensor_tensor(landed[:], products[:, cols], gate0[:, cols], MULT)
+            scatter(b, 0, small, landed[:])
+            weave(2 + b, 2)
+            quantize(2 + b)
+
+        nc.vector.tensor_tensor(
+            scores[:, half].rearrange(pair, g=2),
+            values_of(parts[1])[:].rearrange(pair, g=2),
+            wgo_first[:, second].unsqueeze(1).to_broadcast([P, 2, small]),
+            MULT,
+        )
+        nc.scalar.activation(gate1, scores[:, BANK:], SIGMOID)
+        nc.gpsimd.tensor_tensor(after_quantize, scores[:, half], gate1, MULT)
+        for b, cols in enumerate((first, second)):
+            scatter(b, small, BANK, after_quantize[:, cols])
+
+        nc.scalar.copy(scores[:, BANK:], values_of(parts[2])[:])
+        nc.scalar.activation(gate3, gate3, SIGMOID)
+        nc.gpsimd.tensor_tensor(products[:, half], scores[:, BANK:], wgo_first[:], MULT)
+        nc.gpsimd.tensor_tensor(scores[:, BANK:], products[:, half], gate3, MULT)
+        scatter(2, 0, BANK, scores[:, BANK:])
+
         scaled = weighted_t(2)
-        turns = [gates[:, 2 * BANK :], weighted_early[:]]
-        freed = []
-        for b in range(BLOCKS):
-            if b == 2:
-                keys_sb = out_of_psum(keys_of(1, 2)[:], "keys_late")
-                gate = turns[0]
-                turns.reverse()
-                nc.gpsimd.tensor_tensor(
-                    gate.rearrange("p (g j) -> p g j", g=2),
-                    keys_sb[:].rearrange("p (g j) -> p g j", g=2),
-                    state_of(1, 2, 2, 0, small),
-                    MULT,
-                )
-                values = out_of_psum(multiply(1, 2, psum, "rows", wv_sb, wv_sc, 2, FP4X4)[:], "values_late")
-                nc.scalar.activation(gate, gate, SIGMOID)
-                weigh(1, 2, freed[0][:], values[:])
-                finish(1, 2, 2, 0, small, gate, freed[0][:], values[:])
-            keys = keys_of(2, b)
-            values = turn_back(scaled, b, 1)
-            piece = LAST if b == BLOCKS - 1 else BANK
-            for j0 in range(0, BANK, piece):
-                cols = slice(j0, j0 + piece)
-                gate = turns[0][:, cols]
-                keys_sb = out_of_psum(keys[:, cols], f"keys{b}_{j0}")
-                nc.gpsimd.tensor_tensor(gate, keys_sb[:], state_of(2, b, 1, j0, piece)[:, 0], MULT)
-                weighted = out_of_psum(values[:, cols], f"weighted{b}_{j0}")
-                nc.scalar.activation(gate, gate, SIGMOID)
-                finish(2, b, 1, j0, piece, gate, weighted[:], keys_sb[:])
-                freed.append(weighted)
-            turns.reverse()
+        for b in range(BLOCKS - 1):
+            gate = (gate3, products[:, half])[b % 2]
+            keys_sb = out_of_psum(keys_of([(b, 2)])[:], f"keys{b}")
+            nc.gpsimd.tensor_tensor(gate, keys_sb[:], state_late[:, b, :], MULT)
+            bank = turn_back(scaled, b, 1)
+            if b == 0:
+                weighted = late[:, half]
+                nc.scalar.copy(weighted, bank[:])
+            else:
+                weighted = out_of_psum(bank[:], f"weighted{b}")[:]
+            nc.scalar.activation(gate, gate, SIGMOID)
+            nc.gpsimd.tensor_tensor(keys_sb[:], weighted, gate, MULT)
+            scatter(b, BANK, J, keys_sb[:])
+
+        b = BLOCKS - 1
+        keys_sb = held.tile([P, J], F32, name="keys_last")
+        nc.scalar.copy(keys_sb[:, half], keys_of([(b, 0), (b, 1)])[:])
+        nc.scalar.copy(keys_sb[:, BANK:], keys_of([(b, 2)])[:])
+        nc.gpsimd.tensor_tensor(products[:], keys_sb[:], state_last[:], MULT)
+        values_sb = out_of_psum(values_of([(b, 0), (b, 1)])[:], "values_last")
+        nc.gpsimd.tensor_tensor(late[:, half], values_sb[:], wgo_first[:], MULT)
+        nc.scalar.copy(late[:, BANK:], turn_back(scaled, b, 1)[:])
+        nc.scalar.activation(products[:], products[:], SIGMOID)
+        nc.vector.tensor_tensor(pages[b][:].indirect(places[:]), late[:], products[:], MULT)
+        nc.sync.dma_start(out[b * P :, :], pages[b][:])

@@ -115,11 +115,12 @@ def tile_list_sigS_kernel(
         picked_and_more = held.tile([P, PACK * J + small], F32, name="picked", align_bytes=64)
         picked = picked_and_more[:, : PACK * J].rearrange("p (t j) -> p t j", t=PACK)
         grouped = [picked_and_more[:, PACK * J - small :].bitcast(BF16).rearrange("p (j t) -> p j t", t=PACK)] + [
-            held.tile([P, small, PACK], BF16, name=f"grouped{q}", align_bytes=64)[:] for q in range(1, J // small)
+            held.tile([P, small, PACK], BF16, name=f"grouped{q}", align_bytes=64)[:] for q in (1, 2)
         ]
         codes = [held.tile([P, hi - lo], U32, name=f"codes{lo}", align_bytes=64) for lo, hi in CHUNKS]
         code_sc = [held.tile([P, hi - lo], U8, name=f"code_sc{lo}", align_bytes=64) for lo, hi in CHUNKS]
-        scores = held.tile([P, 2 * BANK], F32, name="scores")
+        scores = held.tile([P, 2 * BANK], F32, name="scores", align_bytes=64)
+        grouped.append(scores[:, :BANK].bitcast(BF16).rearrange("p (j t) -> p j t", t=PACK))
         gates = held.tile([P, 3 * BANK], F32, name="gates")
 
         def gather(i, lo, hi):
@@ -217,9 +218,8 @@ def tile_list_sigS_kernel(
         gather(0, 0, EARLY)
         gather(0, EARLY, J // 2)
         gather(0, J // 2, J)
-        gather(1, 0, J // 2)
-        gather(1, J // 2, J)
-        for q in range(J // small):
+        gather(1, 0, J)
+        for q in range(2):
             weave(q, 0)
         gather(2, 0, J)
         last_plane = PACK - 1
@@ -230,10 +230,10 @@ def tile_list_sigS_kernel(
         gather(last_plane, J - small, J)
         weave(1, 2)
         quantize(1)
+        weave(2, 0)
         first, second, half = slice(0, small), slice(small, BANK), slice(0, BANK)
         products = held.tile([P, J], F32, name="products")
         late = held.tile([P, J], F32, name="late")
-        after_quantize = grouped[-1].rearrange("p j t -> p (j t)").bitcast(F32)
 
         parts = (((0, 0), (1, 0)), ((0, 1), (1, 1)), ((2, 0), (2, 1)))
         values_first = psum_first.tile([P, BANK], F32, name="values_first")
@@ -258,19 +258,26 @@ def tile_list_sigS_kernel(
             nc.gpsimd.tensor_tensor(products[:, cols], landed[:], wgo_first[:, first], MULT)
             nc.gpsimd.tensor_tensor(landed[:], products[:, cols], gate0[:, cols], MULT)
             scatter(b, 0, small, landed[:])
-            weave(2 + b, 2)
-            quantize(2 + b)
+            if b == 0:
+                weave(2, 2)
+                quantize(2)
+        nc.scalar.copy(
+            grouped[-1].rearrange("p (c i) t -> p c t i", i=4),
+            picked[:, :, J - small :].rearrange("p t (c i) -> p c t i", i=4),
+        )
+        quantize(3)
+        weighted_pair = held.tile([P, BANK], F32, name="weighted_pair")
 
         nc.vector.tensor_tensor(
-            scores[:, half].rearrange(pair, g=2),
+            weighted_pair[:].rearrange(pair, g=2),
             values_of(parts[1])[:].rearrange(pair, g=2),
             wgo_first[:, second].unsqueeze(1).to_broadcast([P, 2, small]),
             MULT,
         )
         nc.scalar.activation(gate1, scores[:, BANK:], SIGMOID)
-        nc.gpsimd.tensor_tensor(after_quantize, scores[:, half], gate1, MULT)
+        nc.gpsimd.tensor_tensor(weighted_pair[:], weighted_pair[:], gate1, MULT)
         for b, cols in enumerate((first, second)):
-            scatter(b, small, BANK, after_quantize[:, cols])
+            scatter(b, small, BANK, weighted_pair[:, cols])
 
         nc.scalar.copy(scores[:, BANK:], values_of(parts[2])[:])
         nc.scalar.activation(gate3, gate3, SIGMOID)

@@ -310,4 +310,5 @@ def tile_list_sigS_kernel(
         nc.scalar.copy(late[:, BANK:], turn_back(scaled, b, 1)[:])
         nc.scalar.activation(products[:], products[:], SIGMOID)
         nc.vector.tensor_tensor(pages[b][:].indirect(places[:]), late[:], products[:], MULT)
-        nc.sync.dma_start(out[b * P :, :], pages[b][:])
+        nc.sync.dma_start(out[b * P :, : T // 2], pages[b][:, : T // 2])
+        nc.scalar.dma_start(out[b * P :, T // 2 :], pages[b][:, T // 2 :])

@@ -45,7 +45,6 @@ def tile_list_sigS_kernel(
         wgo_first = held.tile([P, 2 * small], F32, name="wgo_first")
         wgt_rows = held.tile([P, P], F32, name="wgt_rows")
         wgo_rows = held.tile([P, P], F32, name="wgo_rows")
-        wgo_t = held.tile([P, P], F32, name="wgo_t")
         identity = held.tile([P, P], F32, name="identity")
         planes = [held.tile([P, T], F32, name=f"plane{i}") for i in range(PACK)]
         pages = [held.tile([P, T], F32, name=f"page{b}") for b in range(BLOCKS)]
@@ -79,8 +78,7 @@ def tile_list_sigS_kernel(
         nc.sync.dma_start(picks[:], offs)
         for i in range(PACK):
             nc.sync.dma_start(planes[i][:], x_planes[i])
-            if i == 1:
-                nc.sync.dma_start(wgo_rows[:], wgo.rearrange("(h r) (u j) -> r h u j", r=8, j=P)[0])
+        nc.sync.dma_start(wgo_rows[:], wgo.rearrange("(h r) (u j) -> r h u j", r=8, j=P)[0])
         nc.sync.dma_start(wv_sb[:].bitcast(I32), wv_words[0].bitcast(I32))
         nc.sync.dma_start(wk_sb[:].bitcast(I32), wk_words[0].rearrange("p n t -> p (n t)").bitcast(I32))
         nc.sync.dma_start(state_first[:], st_blocks[:, :2, :BANK])
@@ -108,7 +106,7 @@ def tile_list_sigS_kernel(
         for u0, tiles in ((0, 1), (1, 3), (4, 4)):
             bank = spread(turned[:, :P], u0, tiles, wgt_sb, nc.vector.tensor_copy)
         nc.tensor.transpose(bank[:, :P], wgo_rows[:], identity[:])
-        nc.scalar.copy(wgo_t[:], bank[:, :P])
+        wgo_bank = bank
 
         for b in range(BLOCKS):
             nc.gpsimd.memset(pages[b][:], 0.0)
@@ -221,6 +219,8 @@ def tile_list_sigS_kernel(
         gather(1, 0, J)
         for q in range(2):
             weave(q, 0)
+        wgo_t = picked[:, 0, small : small + P]
+        nc.scalar.copy(wgo_t, wgo_bank[:, :P])
         gather(2, 0, J)
         last_plane = PACK - 1
         gather(last_plane, 0, small)

@@ -69,7 +69,6 @@ def tile_list_sigS_kernel(
         nc.scalar.activation(warm[:], warm[:], SIGMOID)
 
         make_identity(nc, identity[:])
-        load_scales(nc.gpsimd, wk_sc, wk_scales)
         load_scales(nc.scalar, wv_sc, wv_scales)
 
         x_planes = xT.rearrange("(p i) t -> i p t", i=PACK)
@@ -108,7 +107,10 @@ def tile_list_sigS_kernel(
         nc.tensor.transpose(bank[:, :P], wgo_rows[:], identity[:])
         wgo_bank = bank
 
-        for b in range(BLOCKS):
+        nc.gpsimd.memset(pages[0][:, :P], 0.0)
+        nc.gpsimd.memset(pages[0][:, P:], 0.0)
+        load_scales(nc.gpsimd, wk_sc, wk_scales)
+        for b in range(1, BLOCKS):
             nc.gpsimd.memset(pages[b][:], 0.0)
         picked_and_more = held.tile([P, PACK * J + small], F32, name="picked", align_bytes=64)
         picked = picked_and_more[:, : PACK * J].rearrange("p (t j) -> p t j", t=PACK)

@@ -307,8 +307,28 @@ def tile_list_sigS_kernel(
         nc.scalar.copy(keys_sb[:, half], keys_of([(b, 0), (b, 1)])[:])
         nc.scalar.copy(keys_sb[:, BANK:], keys_of([(b, 2)])[:])
         nc.gpsimd.tensor_tensor(products[:], keys_sb[:], state_last[:], MULT)
-        values_sb = out_of_psum(values_of([(b, 0), (b, 1)])[:], "values_last")
-        nc.gpsimd.tensor_tensor(late[:, half], values_sb[:], wgo_first[:], MULT)
+        bank = psum.tile([P, BANK], F32, name="rows")
+        scaled_last = held.tile([P, BANK], F32, name="scaled_last")
+        for u in range(BANK // P):
+            c, at = divmod(u * P, small)
+            nc.tensor.matmul_mx(
+                out=bank[:, u * P : (u + 1) * P],
+                lhsT=codes[c][:, at : at + P].bitcast(FP8X4),
+                lhsT_scale=code_sc[c][:, at : at + P],
+                rhs=wv_sb[:, 2 * b * P :].bitcast(FP4X4),
+                rhs_scale=wv_sc[:, b * P :],
+                start=True,
+                stop=True,
+            )
+        for u in range(BANK // P):
+            for g in range(GROUPS):
+                rows = slice(u * P + g * GROUP, u * P + (g + 1) * GROUP)
+                column = 2 * g * (J // P) + u
+                nc.scalar.activation(scaled_last[:, rows], bank[:, rows], COPY, scale=wgo_t[:, column : column + 1])
+        bank = psum.tile([P, BANK], F32, name="rows")
+        for u in range(BANK // P):
+            nc.tensor.transpose(bank[:, u * P : (u + 1) * P], scaled_last[:, u * P : (u + 1) * P], identity[:])
+        nc.scalar.copy(late[:, half], bank[:])
         nc.scalar.copy(late[:, BANK:], turn_back(scaled, b, 1)[:])
         nc.scalar.activation(products[:], products[:], SIGMOID)
         nc.vector.tensor_tensor(pages[b][:].indirect(places[:]), late[:], products[:], MULT)

@@ -292,6 +292,9 @@ def tile_list_sigS_kernel(
             gate = (gate3, products[:, half])[b % 2]
             keys_sb = out_of_psum(keys_of([(b, 2)])[:], f"keys{b}")
             nc.gpsimd.tensor_tensor(gate, keys_sb[:], state_late[:, b, :], MULT)
+            if b == BLOCKS - 2:
+                nc.scalar.activation(gate, gate, SIGMOID)
+                break
             bank = turn_back(scaled, b, 1)
             if b == 0:
                 weighted = late[:, half]
@@ -307,6 +310,9 @@ def tile_list_sigS_kernel(
         nc.scalar.copy(keys_sb[:, half], keys_of([(b, 0), (b, 1)])[:])
         nc.scalar.copy(keys_sb[:, BANK:], keys_of([(b, 2)])[:])
         nc.gpsimd.tensor_tensor(products[:], keys_sb[:], state_last[:], MULT)
+        nc.scalar.copy(keys_sb[:, half], turn_back(scaled, b - 1, 1)[:])
+        nc.vector.tensor_tensor(pages[b - 1][:].indirect(places[:, BANK // 16 :]), keys_sb[:, half], gate, MULT)
+        nc.sync.dma_start(out[(b - 1) * P : b * P, :], pages[b - 1][:])
         bank = psum.tile([P, BANK], F32, name="rows")
         scaled_last = held.tile([P, BANK], F32, name="scaled_last")
         for u in range(BANK // P):

@@ -246,28 +246,32 @@ def tile_list_sigS_kernel(
         keys = [keys_of(part) for part in (parts[0][1:], parts[1], parts[2])]
         gate0, gate1, gate3 = gates[:, half], gates[:, BANK:J], gates[:, J:]
         pair = "p (g j) -> p g j"
+        scores_first = (scores[:, first], gate0[:, second])
         for b, cols in enumerate((first, second)):
             bank = (keys_first, keys[0])[b]
-            nc.vector.tensor_tensor(scores[:, cols], bank[:, first], state_first[:, b, first], MULT)
+            nc.vector.tensor_tensor(scores_first[b], bank[:, first], state_first[:, b, first], MULT)
         nc.vector.tensor_tensor(
             scores[:, BANK:].rearrange(pair, g=2), keys[1][:].rearrange(pair, g=2), state_first[:, :, second], MULT
         )
         nc.vector.tensor_tensor(gate3, keys[2][:], state_third[:], MULT)
 
-        for b, cols in enumerate((first, second)):
-            landed = out_of_psum(values0[b][:, first], f"values{b}")
-            nc.scalar.activation(gate0[:, cols], scores[:, cols], SIGMOID)
-            nc.gpsimd.tensor_tensor(products[:, cols], landed[:], wgo_first[:, first], MULT)
-            nc.gpsimd.tensor_tensor(landed[:], products[:, cols], gate0[:, cols], MULT)
-            scatter(b, 0, small, landed[:])
-            if b == 0:
-                weave(2, 2)
-                quantize(2)
+        landed = [out_of_psum(values0[b][:, first], f"values{b}") for b in range(2)]
+
+        def first_step(b, cols):
+            nc.scalar.activation(gate0[:, cols], scores_first[b], SIGMOID)
+            nc.gpsimd.tensor_tensor(products[:, cols], landed[b][:], wgo_first[:, first], MULT)
+            nc.gpsimd.tensor_tensor(landed[b][:], products[:, cols], gate0[:, cols], MULT)
+            scatter(b, 0, small, landed[b][:])
+
+        first_step(0, first)
+        weave(2, 2)
+        quantize(2)
         nc.scalar.copy(
             grouped[-1].rearrange("p (c i) t -> p c t i", i=4),
             picked[:, :, J - small :].rearrange("p t (c i) -> p c t i", i=4),
         )
         quantize(3)
+        first_step(1, second)
         weighted_pair = held.tile([P, BANK], F32, name="weighted_pair")
 
         nc.vector.tensor_tensor(

from contextlib import ExitStack

import concourse.mybir as mybir
from concourse.masks import make_identity

K, N, T, J = 512, 512, 2048, 1024
P = 128
PACK = 4
BLOCKS = N // P
GROUPS = 8
GROUP = P // GROUPS
BANK = 512
CHUNKS = ((0, 256), (256, 512), (512, 1024))
WEAVE = 256
EARLY = 128
FLOPS = 2 * 2 * K * N * J

F32 = mybir.dt.float32
BF16 = mybir.dt.bfloat16
I32 = mybir.dt.int32
U32 = mybir.dt.uint32
U16 = mybir.dt.uint16
U8 = mybir.dt.uint8
FP8X4 = mybir.dt.float8_e4m3fn_x4
FP4X4 = mybir.dt.float4_e2m1fn_x4
MULT = mybir.AluOpType.mult
SIGMOID = mybir.ActivationFunctionType.Sigmoid
COPY = mybir.ActivationFunctionType.Copy


def tile_list_sigS_kernel(
    tc, xT, wgt, wk_words, wk_scales, wv_words, wv_scales, st, wgo, offs, offs2, out
):
    nc = tc.nc
    with ExitStack() as ctx:
        held = ctx.enter_context(tc.tile_pool(name="held", bufs=1))
        psum = ctx.enter_context(tc.psum_pool(name="psum", bufs=3))
        psum_k = ctx.enter_context(tc.psum_pool(name="psum_k", bufs=3))
        psum_first = ctx.enter_context(tc.psum_pool(name="psum_first", bufs=1))

        small = CHUNKS[0][1]
        picks = held.tile([P, J // 16], U16, name="picks")
        places = held.tile([P, J // 16], U16, name="places")
        wgt_sb = held.tile([P, J], F32, name="wgt_sb")
        wgo_first = held.tile([P, 2 * small], F32, name="wgo_first")
        wgt_rows = held.tile([P, P], F32, name="wgt_rows")
        wgo_rows = held.tile([P, P], F32, name="wgo_rows")
        identity = held.tile([P, P], F32, name="identity")
        planes = [held.tile([P, T], F32, name=f"plane{i}") for i in range(PACK)]
        pages = [held.tile([P, T], F32, name=f"page{b}") for b in range(BLOCKS)]
        state_first = held.tile([P, 2, BANK], F32, name="state_first")
        state_third = held.tile([P, BANK], F32, name="state_third")
        state_late = held.tile([P, BLOCKS - 1, BANK], F32, name="state_late")
        state_last = held.tile([P, J], F32, name="state_last")
        wk_sb = held.tile([P, N], U32, name="wk_sb", align_bytes=64)
        wv_sb = held.tile([P, 2 * N], U8, name="wv_sb", align_bytes=64)
        wk_sc = held.tile([P, N], U8, name="wk_sc", align_bytes=64)
        wv_sc = held.tile([P, N], U8, name="wv_sc", align_bytes=64)

        def load_scales(queue, plane_sc, scales):
            for q in range(4):
                queue.dma_start(
                    plane_sc[32 * q : 32 * q + 4, :].bitcast(I32),
                    scales[0, 4 * q : 4 * q + 4, :].bitcast(I32),
                )

        warm = held.tile([P, 1], F32, name="warm")
        nc.gpsimd.memset(warm[:], 0.0)
        nc.scalar.activation(warm[:], warm[:], SIGMOID)

        make_identity(nc, identity[:])
        load_scales(nc.scalar, wv_sc, wv_scales)

        x_planes = xT.rearrange("(p i) t -> i p t", i=PACK)
        st_blocks = st.rearrange("(b p) j -> p b j", p=P)
        nc.sync.dma_start(wgt_rows[:], wgt.rearrange("(h r) (u j) -> r h u j", r=8, j=P)[0])
        nc.sync.dma_start(picks[:], offs)
        for i in range(PACK):
            nc.sync.dma_start(planes[i][:], x_planes[i])
        nc.sync.dma_start(wgo_rows[:], wgo.rearrange("(h r) (u j) -> r h u j", r=8, j=P)[0])
        nc.sync.dma_start(wv_sb[:].bitcast(I32), wv_words[0].bitcast(I32))
        nc.sync.dma_start(wk_sb[:].bitcast(I32), wk_words[0].rearrange("p n t -> p (n t)").bitcast(I32))
        nc.sync.dma_start(state_first[:], st_blocks[:, :2, :BANK])
        nc.sync.dma_start(wgo_first[:], wgo[:, : 2 * small])
        nc.sync.dma_start(state_third[:], st_blocks[:, 2, :BANK])
        nc.sync.dma_start(places[:], offs2)
        nc.sync.dma_start(state_late[:], st_blocks[:, : BLOCKS - 1, BANK:])
        nc.sync.dma_start(state_last[:], st_blocks[:, BLOCKS - 1, :])

        turned = psum.tile([P, BANK], F32, name="rows")
        nc.tensor.transpose(turned[:, :P], wgt_rows[:], identity[:])

        def spread(columns, u0, tiles, target, copy):
            wide = held.tile([P, tiles, 16, 8], F32, name=f"wide_{target.shape[1]}_{u0}")
            by_tile = columns.rearrange("p (h u) -> p u h", h=16)[:, u0 : u0 + tiles, :]
            copy(wide[:], by_tile.unsqueeze(3).to_broadcast([P, tiles, 16, 8]))
            bank = psum_k.tile([P, BANK], F32, name="keys")
            for u in range(tiles):
                nc.tensor.transpose(
                    bank[:, u * P : (u + 1) * P], wide[:, u].rearrange("p g r -> p (g r)"), identity[:]
                )
            nc.scalar.copy(target[:, u0 * P : (u0 + tiles) * P], bank[:, : tiles * P])
            return bank

        for u0, tiles in ((0, 1), (1, 3), (4, 4)):
            bank = spread(turned[:, :P], u0, tiles, wgt_sb, nc.vector.tensor_copy)
        nc.tensor.transpose(bank[:, :P], wgo_rows[:], identity[:])
        wgo_bank = bank

        nc.gpsimd.memset(pages[0][:, :P], 0.0)
        nc.gpsimd.memset(pages[0][:, P:], 0.0)
        load_scales(nc.gpsimd, wk_sc, wk_scales)
        for b in range(1, BLOCKS):
            nc.gpsimd.memset(pages[b][:], 0.0)
        picked_and_more = held.tile([P, PACK * J + small], F32, name="picked", align_bytes=64)
        picked = picked_and_more[:, : PACK * J].rearrange("p (t j) -> p t j", t=PACK)
        grouped = [picked_and_more[:, PACK * J - small :].bitcast(BF16).rearrange("p (j t) -> p j t", t=PACK)] + [
            held.tile([P, small, PACK], BF16, name=f"grouped{q}", align_bytes=64)[:] for q in (1, 2)
        ]
        codes = [held.tile([P, hi - lo], U32, name=f"codes{lo}", align_bytes=64) for lo, hi in CHUNKS]
        code_sc = [held.tile([P, hi - lo], U8, name=f"code_sc{lo}", align_bytes=64) for lo, hi in CHUNKS]
        scores = held.tile([P, 2 * BANK], F32, name="scores", align_bytes=64)
        grouped.append(scores[:, :BANK].bitcast(BF16).rearrange("p (j t) -> p j t", t=PACK))
        gates = held.tile([P, 3 * BANK], F32, name="gates")

        def gather(i, lo, hi):
            window = planes[i][:].indirect(picks[:, lo // 16 : hi // 16])
            nc.vector.tensor_tensor(picked[:, i, lo:hi], window, wgt_sb[:, lo:hi], MULT)

        def weave(q, i0):
            for j0 in range(0, small, WEAVE):
                nc.scalar.copy(
                    grouped[q][:, j0 : j0 + WEAVE, i0 : i0 + 2].rearrange("p (c i) t -> p c i t", i=4),
                    picked[:, i0 : i0 + 2, q * small + j0 : q * small + j0 + WEAVE].rearrange("p t (c i) -> p c i t", i=4),
                )

        def quantize(q):
            c = min(q, 2)
            cols = slice(q * small - CHUNKS[c][0], (q + 1) * small - CHUNKS[c][0])
            nc.vector.quantize_mx(
                out=codes[c][:, cols].bitcast(FP8X4),
                scales=code_sc[c][:, cols],
                in_=grouped[q].rearrange("p j t -> p (j t)"),
            )

        def multiply(bank, at, b, c, words, scales, size, view):
            lo, hi = CHUNKS[c]
            rows = slice(b * P, (b + 1) * P)
            nc.tensor.matmul_mx(
                out=bank[:, at : at + hi - lo],
                lhsT=words[:, size * rows.start : size * rows.stop].bitcast(view),
                lhsT_scale=scales[:, rows],
                rhs=codes[c][:].bitcast(FP8X4),
                rhs_scale=code_sc[c][:],
                start=True,
                stop=True,
            )

        def keys_of(parts):
            bank = psum_k.tile([P, BANK], F32, name="keys")
            for n, (b, c) in enumerate(parts):
                multiply(bank, n * small, b, c, wk_sb, wk_sc, 1, FP8X4)
            return bank

        def values_of(parts):
            bank = psum.tile([P, BANK], F32, name="rows")
            for n, (b, c) in enumerate(parts):
                multiply(bank, n * small, b, c, wv_sb, wv_sc, 2, FP4X4)
            return bank

        def weighted_t(c):
            lo, hi = CHUNKS[c]
            scaled = [held.tile([P, N], F32, name=f"scaled{u}")[:] for u in range((hi - lo) // P)]
            for u in range((hi - lo) // P):
                entries = slice(u * P, (u + 1) * P)
                bank = psum_k.tile([P, N], F32, name="keys")
                nc.tensor.matmul_mx(
                    out=bank[:],
                    lhsT=codes[c][:, entries].bitcast(FP8X4),
                    lhsT_scale=code_sc[c][:, entries],
                    rhs=wv_sb[:].bitcast(FP4X4),
                    rhs_scale=wv_sc[:],
                    start=True,
                    stop=True,
                )
                for g in range(GROUPS):
                    rows = slice(g * GROUP, (g + 1) * GROUP)
                    column = 2 * g * (J // P) + lo // P + u
                    nc.scalar.activation(
                        scaled[u].rearrange("p (b r) -> p b r", r=P)[:, :, rows],
                        bank[:].rearrange("p (b r) -> p b r", r=P)[:, :, rows],
                        COPY,
                        scale=wgo_t[:, column : column + 1],
                    )
            return scaled

        def turn_back(scaled, b0, group):
            tiles = len(scaled)
            bank = psum.tile([P, BANK], F32, name="rows")
            for g in range(group):
                for u in range(tiles):
                    at = (g * tiles + u) * P
                    nc.tensor.transpose(
                        bank[:, at : at + P], scaled[u][:, (b0 + g) * P : (b0 + g + 1) * P], identity[:]
                    )
            return bank

        def out_of_psum(bank, name):
            landed = held.tile([P, bank.shape[1]], F32, name=name)
            nc.scalar.copy(landed[:], bank)
            return landed

        def scatter(b, lo, hi, gated):
            nc.vector.tensor_copy(pages[b][:].indirect(places[:, lo // 16 : hi // 16]), gated)
            if hi == J:
                nc.sync.dma_start(out[b * P : (b + 1) * P, :], pages[b][:])

        gather(0, 0, EARLY)
        gather(0, EARLY, J // 2)
        gather(0, J // 2, J)
        gather(1, 0, J)
        for q in range(2):
            weave(q, 0)
        wgo_t = picked[:, 0, small : small + P]
        nc.scalar.copy(wgo_t, wgo_bank[:, :P])
        gather(2, 0, J)
        last_plane = PACK - 1
        gather(last_plane, 0, small)
        gather(last_plane, small, J - small)
        weave(0, 2)
        quantize(0)
        gather(last_plane, J - small, J)
        weave(1, 2)
        quantize(1)
        weave(2, 0)
        first, second, half = slice(0, small), slice(small, BANK), slice(0, BANK)
        products = held.tile([P, J], F32, name="products")
        late = held.tile([P, J], F32, name="late")

        parts = (((0, 0), (1, 0)), ((0, 1), (1, 1)), ((2, 0), (2, 1)))
        values_first = psum_first.tile([P, BANK], F32, name="values_first")
        keys_first = psum_first.tile([P, BANK], F32, name="keys_first")
        multiply(values_first, 0, 0, 0, wv_sb, wv_sc, 2, FP4X4)
        multiply(keys_first, 0, 0, 0, wk_sb, wk_sc, 1, FP8X4)
        values0 = (values_first, values_of(parts[0][1:]))
        keys = [keys_of(part) for part in (parts[0][1:], parts[1], parts[2])]
        gate0, gate1, gate3 = gates[:, half], gates[:, BANK:J], gates[:, J:]
        pair = "p (g j) -> p g j"
        scores_first = (scores[:, first], gate0[:, second])
        for b, cols in enumerate((first, second)):
            bank = (keys_first, keys[0])[b]
            nc.vector.tensor_tensor(scores_first[b], bank[:, first], state_first[:, b, first], MULT)
        nc.vector.tensor_tensor(
            scores[:, BANK:].rearrange(pair, g=2), keys[1][:].rearrange(pair, g=2), state_first[:, :, second], MULT
        )
        nc.vector.tensor_tensor(gate3, keys[2][:], state_third[:], MULT)

        landed = [out_of_psum(values0[b][:, first], f"values{b}") for b in range(2)]

        def first_step(b, cols):
            nc.scalar.activation(gate0[:, cols], scores_first[b], SIGMOID)
            nc.gpsimd.tensor_tensor(products[:, cols], landed[b][:], wgo_first[:, first], MULT)
            nc.gpsimd.tensor_tensor(landed[b][:], products[:, cols], gate0[:, cols], MULT)
            scatter(b, 0, small, landed[b][:])

        first_step(0, first)
        weave(2, 2)
        quantize(2)
        nc.scalar.copy(
            grouped[-1].rearrange("p (c i) t -> p c t i", i=4),
            picked[:, :, J - small :].rearrange("p t (c i) -> p c t i", i=4),
        )
        quantize(3)
        first_step(1, second)
        weighted_pair = held.tile([P, BANK], F32, name="weighted_pair")

        nc.vector.tensor_tensor(
            weighted_pair[:].rearrange(pair, g=2),
            values_of(parts[1])[:].rearrange(pair, g=2),
            wgo_first[:, second].unsqueeze(1).to_broadcast([P, 2, small]),
            MULT,
        )
        nc.scalar.activation(gate1, scores[:, BANK:], SIGMOID)
        nc.gpsimd.tensor_tensor(weighted_pair[:], weighted_pair[:], gate1, MULT)
        for b, cols in enumerate((first, second)):
            scatter(b, small, BANK, weighted_pair[:, cols])

        nc.scalar.copy(scores[:, BANK:], values_of(parts[2])[:])
        nc.scalar.activation(gate3, gate3, SIGMOID)
        nc.gpsimd.tensor_tensor(products[:, half], scores[:, BANK:], wgo_first[:], MULT)
        nc.gpsimd.tensor_tensor(scores[:, BANK:], products[:, half], gate3, MULT)
        scatter(2, 0, BANK, scores[:, BANK:])

        scaled = weighted_t(2)
        for b in range(BLOCKS - 1):
            gate = (gate3, products[:, half])[b % 2]
            keys_sb = out_of_psum(keys_of([(b, 2)])[:], f"keys{b}")
            nc.gpsimd.tensor_tensor(gate, keys_sb[:], state_late[:, b, :], MULT)
            if b == BLOCKS - 2:
                nc.scalar.activation(gate, gate, SIGMOID)
                break
            bank = turn_back(scaled, b, 1)
            if b == 0:
                weighted = late[:, half]
                nc.scalar.copy(weighted, bank[:])
            else:
                weighted = out_of_psum(bank[:], f"weighted{b}")[:]
            nc.scalar.activation(gate, gate, SIGMOID)
            nc.gpsimd.tensor_tensor(keys_sb[:], weighted, gate, MULT)
            scatter(b, BANK, J, keys_sb[:])

        b = BLOCKS - 1
        keys_sb = held.tile([P, J], F32, name="keys_last")
        nc.scalar.copy(keys_sb[:, half], keys_of([(b, 0), (b, 1)])[:])
        nc.scalar.copy(keys_sb[:, BANK:], keys_of([(b, 2)])[:])
        nc.gpsimd.tensor_tensor(products[:], keys_sb[:], state_last[:], MULT)
        nc.scalar.copy(keys_sb[:, half], turn_back(scaled, b - 1, 1)[:])
        nc.vector.tensor_tensor(pages[b - 1][:].indirect(places[:, BANK // 16 :]), keys_sb[:, half], gate, MULT)
        nc.sync.dma_start(out[(b - 1) * P : b * P, :], pages[b - 1][:])
        bank = psum.tile([P, BANK], F32, name="rows")
        scaled_last = held.tile([P, BANK], F32, name="scaled_last")
        for u in range(BANK // P):
            c, at = divmod(u * P, small)
            nc.tensor.matmul_mx(
                out=bank[:, u * P : (u + 1) * P],
                lhsT=codes[c][:, at : at + P].bitcast(FP8X4),
                lhsT_scale=code_sc[c][:, at : at + P],
                rhs=wv_sb[:, 2 * b * P :].bitcast(FP4X4),
                rhs_scale=wv_sc[:, b * P :],
                start=True,
                stop=True,
            )
        for u in range(BANK // P):
            for g in range(GROUPS):
                rows = slice(u * P + g * GROUP, u * P + (g + 1) * GROUP)
                column = 2 * g * (J // P) + u
                nc.scalar.activation(scaled_last[:, rows], bank[:, rows], COPY, scale=wgo_t[:, column : column + 1])
        bank = psum.tile([P, BANK], F32, name="rows")
        for u in range(BANK // P):
            nc.tensor.transpose(bank[:, u * P : (u + 1) * P], scaled_last[:, u * P : (u + 1) * P], identity[:])
        nc.scalar.copy(late[:, half], bank[:])
        nc.scalar.copy(late[:, BANK:], turn_back(scaled, b, 1)[:])
        nc.scalar.activation(products[:], products[:], SIGMOID)
        nc.vector.tensor_tensor(pages[b][:].indirect(places[:]), late[:], products[:], MULT)
        nc.sync.dma_start(out[b * P :, : T // 2], pages[b][:, : T // 2])
        nc.scalar.dma_start(out[b * P :, T // 2 :], pages[b][:, T // 2 :])
